import numpy as np
import ml_dtypes


def mxq(x, axis, fmt="e4m3"):
    dtype, down = {"e4m3": (ml_dtypes.float8_e4m3fn, 7), "e5m2": (ml_dtypes.float8_e5m2, 14)}[fmt]
    v = np.moveaxis(np.asarray(x, np.float32).astype(ml_dtypes.bfloat16).astype(np.float64), axis, -1)
    blocks = v.reshape(v.shape[:-1] + (-1, 32))
    amax = np.abs(blocks).max(-1, keepdims=True)
    byte = np.maximum(np.where(amax > 0, np.frexp(amax)[1] - 1 + 127, 0) - down, 1)
    scale = np.exp2(byte - 127.0)
    codes = (blocks / scale).astype(np.float32).astype(dtype).astype(np.float64)
    return np.moveaxis((codes * scale).reshape(v.shape), -1, axis)


WIDE = False


def mx_kscale(k):
    if not WIDE:
        return np.ones(k)
    levels = np.array([10, -10, 5, -5, 0])
    if k % 512:
        return np.exp2(np.random.permutation(np.resize(levels, k // 32))).repeat(32)
    a = np.empty((k // 512, 16))
    for p in range(k // 512):
        a[p, :8] = np.random.permutation(np.resize(levels, 8))
        for g in range(8):
            far = levels[np.abs(levels - a[p, g]) >= 10]
            a[p, g + 8] = far[np.random.randint(len(far))]
    return np.exp2(a.ravel()).repeat(32)


BF16 = ml_dtypes.bfloat16


def bf(x):
    return np.asarray(x, np.float32).astype(BF16)


def f64(x):
    return np.asarray(x).astype(np.float64)


E2M1 = np.array([0.0, 0.5, 1.0, 1.5, 2.0, 3.0, 4.0, 6.0, -0.0, -0.5, -1.0, -1.5, -2.0, -3.0, -4.0, -6.0])


def pack_weight(w, fmt):
    k, n = w.shape
    w = f64(bf(w)).reshape(k // 32, 32, n)
    amax = np.abs(w).max(1)
    if fmt == "e4m3":
        byte = np.frexp(amax)[1] - 1 + 127 - 7
    else:
        mant, ex = np.frexp(amax / 6.0)
        byte = np.where(mant > 0.5, ex, ex - 1) + 127
    byte = np.clip(np.where(amax > 0, byte, 1), 1, 254)
    scaled = (w * np.exp2(127.0 - byte)[:, None, :]).reshape(k, n).astype(np.float32)
    by_word = np.ascontiguousarray(scaled.reshape(k // 512, 128, 4, n).transpose(0, 1, 3, 2))
    if fmt == "e4m3":
        words = by_word.astype(ml_dtypes.float8_e4m3fn).view(np.uint8)
    else:
        c = by_word.astype(ml_dtypes.float4_e2m1fn).view(np.uint8) & 0xF
        words = c[..., 0::2] | (c[..., 1::2] << 4)
    return np.ascontiguousarray(words), np.ascontiguousarray(byte.astype(np.uint8).reshape(k // 512, 16, n))


def unpack_weight(words, scales, fmt):
    g, p, n, _ = words.shape
    if fmt == "e4m3":
        vals = np.ascontiguousarray(words).view(ml_dtypes.float8_e4m3fn).astype(np.float64)
    else:
        nib = np.empty((g, p, n, 4), np.uint8)
        nib[..., 0::2] = words & 0xF
        nib[..., 1::2] = words >> 4
        vals = E2M1[nib]
    vals = vals * np.repeat(np.exp2(scales.astype(np.float64) - 127.0), 8, axis=1)[..., None]
    return vals.transpose(0, 1, 3, 2).reshape(g * 512, n)
def pack4(w):
    words, scales = pack_weight(w, "e2m1")
    return words.reshape(words.shape[0], 128, -1), scales


def unpack4(words, scales):
    return unpack_weight(words.reshape(words.shape[0], 128, -1, 2), scales, "e2m1")


C, K, J, M = 2048, 1024, 1024, 512


def draw0():
    s = mx_kscale(K)
    t = mx_kscale(C)
    tastes = np.random.standard_normal((C, K)) * s
    chars = 0.7 * np.random.standard_normal((K, J)) / np.sqrt(K) / s[:, None]
    delta = 0.3 * np.random.standard_normal(J)
    inv_denom = np.random.uniform(0.5, 1.5, C) * t
    demo = np.random.standard_normal((C, M)) / np.sqrt(C) / t[:, None]
    demo_words, demo_scales = pack4(demo)
    return {"tastes": bf(tastes), "chars": bf(chars), "delta": bf(delta), "inv_denom": bf(inv_denom),
            "demo_words": demo_words, "demo_scales": demo_scales}


def core(tastes, chars, delta, inv_denom, demo_words, demo_scales):
    mu = mxq(f64(tastes), 1, "e4m3") @ mxq(f64(chars), 0, "e4m3")
    share = np.exp(mu + f64(delta)) * f64(inv_denom)[:, None]
    demo = unpack4(demo_words, demo_scales)
    return demo.T @ mxq(share, 0, "e4m3")


def e4m3fn_bytes(y):
    return np.clip(np.asarray(y, np.float64), -448.0, 448.0).astype(np.float32).astype(ml_dtypes.float8_e4m3fn).view(np.uint8)


def e4m3fn_values(b):
    return np.asarray(b, np.uint8).view(ml_dtypes.float8_e4m3fn).astype(np.float64)


def setup_inputs():
    d = draw0()
    x0 = np.asarray(d['tastes']).astype(np.float64)
    s = (np.max(np.abs(x0), axis=(0,), keepdims=True) / 448.0).astype(np.float32)
    out = {}
    for k, v in d.items():
        if k == 'tastes':
            out['tastes_bytes'] = e4m3fn_bytes(x0 / s.astype(np.float64))
            out['tastes_scale'] = s
        else:
            out[k] = v
    return out


def reference(tastes_bytes, tastes_scale, chars, delta, inv_denom, demo_words, demo_scales):
    return core(e4m3fn_values(tastes_bytes) * tastes_scale.astype(np.float64), chars, delta, inv_denom, demo_words, demo_scales)

@@ -1,0 +1,291 @@
+import math
+from contextlib import ExitStack
+
+import concourse.mybir as mybir
+from concourse.masks import make_identity
+
+C, K, J, M = 2048, 1024, 1024, 512
+FLOPS = 2 * C * K * J + 2 * C * M * J
+
+F32 = mybir.dt.float32
+BF16 = mybir.dt.bfloat16
+I32 = mybir.dt.int32
+U32 = mybir.dt.uint32
+U8 = mybir.dt.uint8
+E4M3 = mybir.dt.float8_e4m3fn
+E4M3X4 = mybir.dt.float8_e4m3fn_x4
+E2M1X4 = mybir.dt.float4_e2m1fn_x4
+ALU = mybir.AluOpType
+ACT = mybir.ActivationFunctionType
+
+P = 128
+GROUPS = C // 512
+TILES = C // P
+JH = 512
+LN2 = math.log(2.0)
+
+
+def tile_blp_choice_micro_moments_s13_kernel(
+    tc, tastes_bytes, tastes_scale, chars, delta, inv_denom, demo_words, demo_scales, out
+):
+    nc = tc.nc
+    with ExitStack() as ctx:
+        keep = ctx.enter_context(tc.tile_pool(name="keep", bufs=1))
+        ring = ctx.enter_context(tc.tile_pool(name="ring", bufs=2))
+        psum = ctx.enter_context(tc.psum_pool(name="psum", bufs=1))
+        ctx.enter_context(tc.manual_schedule())
+
+        ident = keep.tile([P, P], F32, name="ident")
+        make_identity(nc, ident[:])
+        dscale = keep.tile([P, GROUPS, M], U8, name="dscale", align_bytes=64)
+        nc.gpsimd.memset(dscale[:].rearrange("p g m -> p (g m)").bitcast(I32), 0)
+
+        inv = keep.tile([P, GROUPS, 4], BF16, name="inv")
+        nc.sync.dma_start(out=inv[:], in_=inv_denom.rearrange("(g p t) -> p g t", p=P, t=4))
+
+        t_view = tastes_bytes.rearrange("(g p t) k -> g p t k", p=P, t=4)
+        raw = [keep.tile([P, 4, K], U8, name="raw%d" % g, align_bytes=64) for g in range(GROUPS)]
+        scale = keep.tile([P, K], F32, name="scale", align_bytes=64)
+        c_view = chars.rearrange("(g p t) j -> g p t j", p=P, t=4)
+        craw = [[keep.tile([P, 4, JH], BF16, name="craw%d%d" % (g, h), align_bytes=64) for h in range(2)] for g in range(2)]
+        delta_bc = keep.tile([P, J], BF16, name="delta_bc", align_bytes=64)
+        dwords = keep.tile([P, GROUPS, 2 * M], U8, name="dwords", align_bytes=64)
+
+        nc.sync.dma_start(out=raw[0][:, 0:1, :], in_=t_view[0][:, 0:1, :])
+        nc.scalar.dma_start(out=scale[:], in_=tastes_scale.rearrange("o k -> (o k)").partition_broadcast(P))
+        nc.sync.dma_start(out=raw[0][:, 1:4, :], in_=t_view[0][:, 1:4, :])
+        nc.sync.dma_start(out=craw[0][0][:], in_=c_view[0][:, :, 0:JH])
+        nc.sync.dma_start(out=craw[1][0][:], in_=c_view[1][:, :, 0:JH])
+        nc.sync.dma_start(out=raw[1][:], in_=t_view[1])
+        nc.sync.dma_start(out=delta_bc[:], in_=delta.partition_broadcast(P))
+        nc.sync.dma_start(out=craw[0][1][:], in_=c_view[0][:, :, JH:J])
+        nc.sync.dma_start(out=craw[1][1][:], in_=c_view[1][:, :, JH:J])
+        nc.sync.dma_start(out=raw[2][:], in_=t_view[2])
+        nc.sync.dma_start(out=raw[3][:], in_=t_view[3])
+        nc.sync.dma_start(
+            out=dwords[:].rearrange("p g n -> p (g n)").bitcast(I32).rearrange("p (g n) -> p g n", g=GROUPS),
+            in_=demo_words.bitcast(I32).rearrange("g p n -> p g n"),
+        )
+        for q in range(4):
+            nc.sync.dma_start(
+                out=dscale[32 * q : 32 * q + 4, :, :].rearrange("p g m -> p (g m)").bitcast(I32).rearrange("p (g m) -> p g m", g=GROUPS),
+                in_=demo_scales.bitcast(I32).rearrange("g q m -> q g m")[4 * q : 4 * q + 4, :, :],
+            )
+
+        inv32 = keep.tile([P, TILES], F32, name="inv32")
+        nc.vector.tensor_copy(out=inv32[:], in_=inv[:].rearrange("p g t -> p (g t)"))
+        expo = keep.tile([P, TILES], I32, name="expo")
+        sig = keep.tile([P, TILES], I32, name="sig")
+        nc.vector.tensor_scalar(expo[:], inv32[:].bitcast(I32), 23, None, ALU.logical_shift_right)
+        nc.vector.tensor_scalar(sig[:], inv32[:].bitcast(I32), 0x7FFFFF, 0x3F800000, ALU.bitwise_and, ALU.bitwise_or)
+        expo32 = keep.tile([P, TILES], F32, name="expo32")
+        nc.vector.tensor_copy(out=expo32[:], in_=expo[:])
+        lnsig = keep.tile([P, TILES], F32, name="lnsig")
+        nc.scalar.activation(lnsig[:], sig[:].bitcast(F32), ACT.Ln)
+        expo_ln = keep.tile([P, TILES], F32, name="expo_ln")
+        nc.vector.tensor_scalar(expo_ln[:], expo32[:], -127.0, LN2, ALU.add, ALU.mult)
+        lninv = keep.tile([P, TILES], F32, name="lninv")
+
+        wid = {}
+        xts = {}
+        pairs = {}
+        tcodes = [keep.tile([P, 2 * 256], U32, name="tcodes%d" % q, align_bytes=64) for q in range(TILES // 2)]
+        tscales = [keep.tile([P, 2 * 256], U8, name="tscales%d" % q, align_bytes=64) for q in range(TILES // 2)]
+        cgrp = [[keep.tile([P, JH, 4], BF16, name="cgrp%d%d" % (g, h), align_bytes=64) for h in range(2)] for g in range(2)]
+        ccodes = [[keep.tile([P, JH], U32, name="ccodes%d%d" % (g, h), align_bytes=64) for h in range(2)] for g in range(2)]
+        cscales = [[keep.tile([P, JH], U8, name="cscales%d%d" % (g, h), align_bytes=64) for h in range(2)] for g in range(2)]
+
+        def widen(n):
+            w = ring.tile([P, K], BF16, name="wid", tag="wid", bufs=4, align_bytes=64)
+            nc.vector.tensor_tensor(w[:], raw[n // 4][:, n % 4, :].bitcast(E4M3), scale[:], ALU.mult)
+            wid[n] = w
+
+        def turn(n):
+            x = psum.tile([P, 2, 2, P], F32, name="xt", tag="xt", bufs=2)
+            words = wid[n][:].bitcast(F32)
+            for g in range(2):
+                for u in range(2):
+                    nc.tensor.transpose(x[:, g, u, :], words[:, 256 * g + u : 256 * (g + 1) : 2], ident[:])
+            xts[n] = x
+
+        def gather(n):
+            q, e = divmod(n, 2)
+            if e == 0:
+                pairs[q] = ring.tile([P, 2 * K], BF16, name="pair", tag="pair", bufs=3, align_bytes=64)
+            dst = pairs[q][:, e * K : (e + 1) * K].bitcast(F32).rearrange("p (g r u) -> p g r u", g=2, u=2)
+            nc.scalar.copy(out=dst, in_=xts[n][:].rearrange("p g u r -> p g r u"))
+
+        def quant_tastes(q):
+            nc.vector.quantize_mx(out=tcodes[q][:].bitcast(E4M3X4), scales=tscales[q][:], in_=pairs[q][:])
+
+        def interleave_chars(g, h, half):
+            cols = slice(256 * half, 256 * (half + 1))
+            nc.scalar.copy(
+                out=cgrp[g][h][:, cols, :].rearrange("p (c i) t -> p c t i", i=4),
+                in_=craw[g][h][:, :, cols].rearrange("p t (c i) -> p c t i", i=4),
+            )
+
+        def quant_chars(g, h):
+            nc.vector.quantize_mx(
+                out=ccodes[g][h][:].bitcast(E4M3X4), scales=cscales[g][h][:], in_=cgrp[g][h][:].rearrange("p j t -> p (j t)")
+            )
+
+        mus = {}
+        xs = {}
+        shares = {}
+        scodes = {}
+        accs = {}
+
+        def first_product(s):
+            h, n = divmod(s, TILES)
+            tag = "mu" if s < 16 or s % 4 >= 2 else "xt"
+            mu = psum.tile([P, JH], F32, name="mu", tag=tag, bufs=2)
+            q, e = divmod(n, 2)
+            for g in range(2):
+                cols = slice(256 * e + 128 * g, 256 * e + 128 * (g + 1))
+                nc.tensor.matmul_mx(
+                    out=mu[:],
+                    lhsT=tcodes[q][:, cols].bitcast(E4M3X4),
+                    lhsT_scale=tscales[q][:, cols],
+                    rhs=ccodes[g][h][:].bitcast(E4M3X4),
+                    rhs_scale=cscales[g][h][:],
+                    start=(g == 0),
+                    stop=(g == 1),
+                )
+            mus[s] = mu
+
+        def add_logs(s, cols=slice(0, JH)):
+            h, n = divmod(s, TILES)
+            if n % 4 == 0 and cols.start == 0:
+                xs[s // 4] = ring.tile([P, 4, JH], F32, name="xsum", tag="xsum", bufs=2, align_bytes=64)
+            nc.vector.scalar_tensor_tensor(
+                out=xs[s // 4][:, n % 4, cols],
+                in0=mus[s][:, cols],
+                scalar=lninv[:, n : n + 1],
+                in1=delta_bc[:, h * JH + cols.start : h * JH + cols.stop],
+                op0=ALU.add,
+                op1=ALU.add,
+            )
+
+        def exponentiate(b, half):
+            if half == 0:
+                shares[b] = ring.tile([P, JH, 4], BF16, name="share", tag="share", bufs=2, align_bytes=64)
+            cols = slice(256 * half, 256 * (half + 1))
+            nc.scalar.activation(
+                shares[b][:, cols, :].rearrange("p (c i) t -> p c t i", i=4),
+                xs[b][:, :, cols].rearrange("p t (c i) -> p c t i", i=4),
+                ACT.Exp,
+            )
+
+        def quant_share(b, halves=(0, 2)):
+            if halves[0] == 0:
+                codes = ring.tile([P, JH], U32, name="scodes", tag="scodes", bufs=3, align_bytes=64)
+                planes = ring.tile([P, JH], U8, name="splanes", tag="splanes", bufs=3, align_bytes=64)
+                scodes[b] = (codes, planes)
+            codes, planes = scodes[b]
+            cols = slice(256 * halves[0], 256 * halves[1])
+            nc.vector.quantize_mx(
+                out=codes[:, cols].bitcast(E4M3X4),
+                scales=planes[:, cols],
+                in_=shares[b][:, cols, :].rearrange("p j t -> p (j t)"),
+            )
+
+        def second_product(b, m):
+            h, g = divmod(b, GROUPS)
+            if g == 0:
+                accs[h, m] = psum.tile([P, JH], F32, name="acc%d" % m, tag="acc%d" % m, bufs=1)
+            codes, planes = scodes[b]
+            nc.tensor.matmul_mx(
+                out=accs[h, m][:],
+                lhsT=dwords[:, g, 2 * P * m : 2 * P * (m + 1)].bitcast(E2M1X4),
+                lhsT_scale=dscale[:, g, P * m : P * (m + 1)],
+                rhs=codes[:].bitcast(E4M3X4),
+                rhs_scale=planes[:],
+                start=(g == 0),
+                stop=(g == GROUPS - 1),
+            )
+
+        def store(h, m, engine):
+            res = ring.tile([P, JH], F32, name="res", tag="res", bufs=8, align_bytes=64)
+            if engine == "scalar":
+                nc.scalar.copy(out=res[:], in_=accs[h, m][:])
+            else:
+                nc.vector.tensor_copy(out=res[:], in_=accs[h, m][:])
+            nc.sync.dma_start(out=out[P * m : P * (m + 1), h * JH : (h + 1) * JH], in_=res[:])
+
+        for n in range(6):
+            if n == 4:
+                quant_tastes(0)
+            if n == 5:
+                quant_chars(0, 0)
+                quant_tastes(1)
+            widen(n)
+            if n == 0:
+                nc.vector.tensor_tensor(lninv[:], lnsig[:], expo_ln[:], ALU.add)
+            if n < 5:
+                turn(n)
+                gather(n)
+            if n < 4:
+                interleave_chars(n // 2, 0, n % 2)
+        quant_chars(1, 0)
+        first_product(0)
+        first_product(1)
+
+        nxt = 2
+        for s in range(32):
+            last = s >= 28
+            if not last:
+                add_logs(s)
+            elif s == 28:
+                for half in range(2):
+                    for i in range(4):
+                        add_logs(28 + i, slice(256 * half, 256 * (half + 1)))
+                    exponentiate(7, half)
+                    if half == 0:
+                        quant_share(6)
+            if s + 6 < TILES:
+                widen(s + 6)
+            if s % 2 == 1 and (s + 3) // 2 < TILES // 2:
+                quant_tastes((s + 3) // 2)
+            if s == 9 or s == 11:
+                quant_chars((s - 9) // 2, 1)
+            if s < 16:
+                if s % 4 == 2 and s >= 6:
+                    quant_share(s // 4 - 1)
+            else:
+                if s % 4 == 2 and s < 28:
+                    quant_share(s // 4 - 1)
+            if last and s == 30:
+                quant_share(7, (0, 1))
+                quant_share(7, (1, 2))
+            if s + 5 < TILES:
+                turn(s + 5)
+            if s >= 7:
+                b = (s - 7) // 4
+                second_product(b, (s - 7) % 4)
+            target = s + 2 if s < 13 else s + 4
+            while nxt <= min(target, 31):
+                first_product(nxt)
+                nxt += 1
+            if s < 16:
+                if s >= 4 and s % 4 < 2:
+                    exponentiate(s // 4 - 1, s % 4)
+                if s + 5 < TILES:
+                    gather(s + 5)
+                if s in (2, 3, 6, 7):
+                    i = (2, 3, 6, 7).index(s)
+                    interleave_chars(i // 2, 1, i % 2)
+            if s == 16:
+                exponentiate(3, 0)
+                exponentiate(3, 1)
+            if s > 16 and s % 4 == 3 and s < 28:
+                exponentiate(s // 4, 0)
+                exponentiate(s // 4, 1)
+            if s == 22:
+                for m in range(4):
+                    store(0, m, "scalar")
+        for i in range(25, 32):
+            b, m = divmod(i, 4)
+            second_product(b, m)
+        for m in range(4):
+            store(1, m, "scalar" if m % 2 else "vector")

@@ -35,24 +35,28 @@ def tile_blp_choice_micro_moments_s13_kernel(
         psum = ctx.enter_context(tc.psum_pool(name="psum", bufs=1))
         ctx.enter_context(tc.manual_schedule())
 
+        inv_rows = keep.tile([P, 512], BF16, name="inv_rows", align_bytes=64)
+        nc.vector.memset(inv_rows[:], 0.0)
+        one = keep.tile([P, 1], F32, name="one")
+        nc.vector.memset(one[:], 1.0)
         ident = keep.tile([P, P], F32, name="ident")
         make_identity(nc, ident[:])
         dscale = keep.tile([P, GROUPS, M], U8, name="dscale", align_bytes=64)
         nc.gpsimd.memset(dscale[:].rearrange("p g m -> p (g m)").bitcast(I32), 0)
 
-        inv = keep.tile([P, GROUPS, 4], BF16, name="inv")
-        nc.sync.dma_start(out=inv[:], in_=inv_denom.rearrange("(g p t) -> p g t", p=P, t=4))
-
         t_view = tastes_bytes.rearrange("(g p t) k -> g p t k", p=P, t=4)
         raw = [keep.tile([P, 4, K], U8, name="raw%d" % g, align_bytes=64) for g in range(GROUPS)]
         scale = keep.tile([P, K], F32, name="scale", align_bytes=64)
+        scale_row = tastes_scale.rearrange("o k -> (o k)")
         c_view = chars.rearrange("(g p t) j -> g p t j", p=P, t=4)
         craw = [[keep.tile([P, 4, JH], BF16, name="craw%d%d" % (g, h), align_bytes=64) for h in range(2)] for g in range(2)]
         delta_bc = keep.tile([P, J], BF16, name="delta_bc", align_bytes=64)
         dwords = keep.tile([P, GROUPS, 2 * M], U8, name="dwords", align_bytes=64)
 
+        nc.scalar.dma_start(out=scale[:, 0:512], in_=scale_row[0:512].partition_broadcast(P))
         nc.sync.dma_start(out=raw[0][:, 0:1, :], in_=t_view[0][:, 0:1, :])
-        nc.scalar.dma_start(out=scale[:], in_=tastes_scale.rearrange("o k -> (o k)").partition_broadcast(P))
+        nc.sync.dma_start(out=inv_rows[0:GROUPS, :], in_=inv_denom.rearrange("(g r) -> g r", g=GROUPS))
+        nc.sync.dma_start(out=scale[:, 512:1024], in_=scale_row[512:1024].partition_broadcast(P))
         nc.sync.dma_start(out=raw[0][:, 1:4, :], in_=t_view[0][:, 1:4, :])
         nc.sync.dma_start(out=craw[0][0][:], in_=c_view[0][:, :, 0:JH])
         nc.sync.dma_start(out=craw[1][0][:], in_=c_view[1][:, :, 0:JH])
@@ -72,18 +76,25 @@ def tile_blp_choice_micro_moments_s13_kernel(
                 in_=demo_scales.bitcast(I32).rearrange("g q m -> q g m")[4 * q : 4 * q + 4, :, :],
             )
 
+        scrap = keep.tile([P, 1], F32, name="scrap")
+        nc.scalar.activation(scrap[:], one[:], ACT.Ln)
+        inv_t = psum.tile([P, 2, P], F32, name="inv_t", tag="mu", bufs=2)
+        for u in range(2):
+            nc.tensor.transpose(inv_t[:, u, :], inv_rows[:].bitcast(F32)[:, u:256:2], ident[:])
         inv32 = keep.tile([P, TILES], F32, name="inv32")
-        nc.vector.tensor_copy(out=inv32[:], in_=inv[:].rearrange("p g t -> p (g t)"))
+        nc.vector.tensor_copy(
+            out=inv32[:].rearrange("p (g u e) -> p u g e", u=2, e=2),
+            in_=inv_t[:, :, 0:GROUPS].bitcast(BF16).rearrange("p u (g e) -> p u g e", e=2),
+        )
         expo = keep.tile([P, TILES], I32, name="expo")
         sig = keep.tile([P, TILES], I32, name="sig")
-        nc.vector.tensor_scalar(expo[:], inv32[:].bitcast(I32), 23, None, ALU.logical_shift_right)
         nc.vector.tensor_scalar(sig[:], inv32[:].bitcast(I32), 0x7FFFFF, 0x3F800000, ALU.bitwise_and, ALU.bitwise_or)
-        expo32 = keep.tile([P, TILES], F32, name="expo32")
-        nc.vector.tensor_copy(out=expo32[:], in_=expo[:])
+        nc.vector.tensor_scalar(expo[:], inv32[:].bitcast(I32), 23, None, ALU.logical_shift_right)
         lnsig = keep.tile([P, TILES], F32, name="lnsig")
         nc.scalar.activation(lnsig[:], sig[:].bitcast(F32), ACT.Ln)
+        nc.scalar.activation(scrap[:], one[:], ACT.Exp)
         expo_ln = keep.tile([P, TILES], F32, name="expo_ln")
-        nc.vector.tensor_scalar(expo_ln[:], expo32[:], -127.0, LN2, ALU.add, ALU.mult)
+        nc.vector.tensor_scalar(expo_ln[:], expo[:], -127.0, LN2, ALU.add, ALU.mult)
         lninv = keep.tile([P, TILES], F32, name="lninv")
 
         wid = {}
@@ -95,9 +106,12 @@ def tile_blp_choice_micro_moments_s13_kernel(
         ccodes = [[keep.tile([P, JH], U32, name="ccodes%d%d" % (g, h), align_bytes=64) for h in range(2)] for g in range(2)]
         cscales = [[keep.tile([P, JH], U8, name="cscales%d%d" % (g, h), align_bytes=64) for h in range(2)] for g in range(2)]
 
-        def widen(n):
+        def widen(n, pieces=1):
             w = ring.tile([P, K], BF16, name="wid", tag="wid", bufs=4, align_bytes=64)
-            nc.vector.tensor_tensor(w[:], raw[n // 4][:, n % 4, :].bitcast(E4M3), scale[:], ALU.mult)
+            step = K // pieces
+            for i in range(pieces):
+                cols = slice(step * i, step * (i + 1))
+                nc.vector.tensor_tensor(w[:, cols], raw[n // 4][:, n % 4, cols].bitcast(E4M3), scale[:, cols], ALU.mult)
             wid[n] = w
 
         def turn(n):
@@ -135,6 +149,8 @@ def tile_blp_choice_micro_moments_s13_kernel(
         shares = {}
         scodes = {}
         accs = {}
+        whole = ((0, 256), (256, 512))
+        fine = ((0, 256), (256, 384), (384, 512))
 
         def first_product(s):
             h, n = divmod(s, TILES)
@@ -154,40 +170,36 @@ def tile_blp_choice_micro_moments_s13_kernel(
                 )
             mus[s] = mu
 
-        def add_logs(s, cols=slice(0, JH)):
+        def add_logs(s, lo=0, hi=JH):
             h, n = divmod(s, TILES)
-            if n % 4 == 0 and cols.start == 0:
-                xs[s // 4] = ring.tile([P, 4, JH], F32, name="xsum", tag="xsum", bufs=2, align_bytes=64)
+            b = s // 4
+            if n % 4 == 0:
+                xs[b, lo] = ring.tile([P, 4, hi - lo], F32, name="xsum", tag="xsum%d" % (hi - lo), bufs=3 if hi - lo == JH else 2, align_bytes=64)
             nc.vector.scalar_tensor_tensor(
-                out=xs[s // 4][:, n % 4, cols],
-                in0=mus[s][:, cols],
+                out=xs[b, lo][:, n % 4, :],
+                in0=mus[s][:, lo:hi],
                 scalar=lninv[:, n : n + 1],
-                in1=delta_bc[:, h * JH + cols.start : h * JH + cols.stop],
+                in1=delta_bc[:, h * JH + lo : h * JH + hi],
                 op0=ALU.add,
                 op1=ALU.add,
             )
 
-        def exponentiate(b, half):
-            if half == 0:
-                shares[b] = ring.tile([P, JH, 4], BF16, name="share", tag="share", bufs=2, align_bytes=64)
-            cols = slice(256 * half, 256 * (half + 1))
+        def exponentiate(b, lo, hi):
+            if lo == 0:
+                shares[b] = ring.tile([P, JH, 4], BF16, name="share", tag="share", bufs=3, align_bytes=64)
+            x = xs[b, lo][:] if (b, lo) in xs and b == 7 else xs[b, 0][:, :, lo:hi]
             nc.scalar.activation(
-                shares[b][:, cols, :].rearrange("p (c i) t -> p c t i", i=4),
-                xs[b][:, :, cols].rearrange("p t (c i) -> p c t i", i=4),
-                ACT.Exp,
+                shares[b][:, lo:hi, :].rearrange("p (c i) t -> p c t i", i=4), x.rearrange("p t (c i) -> p c t i", i=4), ACT.Exp
             )
 
-        def quant_share(b, halves=(0, 2)):
-            if halves[0] == 0:
+        def quant_share(b, lo, hi):
+            if lo == 0:
                 codes = ring.tile([P, JH], U32, name="scodes", tag="scodes", bufs=3, align_bytes=64)
                 planes = ring.tile([P, JH], U8, name="splanes", tag="splanes", bufs=3, align_bytes=64)
                 scodes[b] = (codes, planes)
             codes, planes = scodes[b]
-            cols = slice(256 * halves[0], 256 * halves[1])
             nc.vector.quantize_mx(
-                out=codes[:, cols].bitcast(E4M3X4),
-                scales=planes[:, cols],
-                in_=shares[b][:, cols, :].rearrange("p j t -> p (j t)"),
+                out=codes[:, lo:hi].bitcast(E4M3X4), scales=planes[:, lo:hi], in_=shares[b][:, lo:hi, :].rearrange("p j t -> p (j t)")
             )
 
         def second_product(b, m):
@@ -219,7 +231,7 @@ def tile_blp_choice_micro_moments_s13_kernel(
             if n == 5:
                 quant_chars(0, 0)
                 quant_tastes(1)
-            widen(n)
+            widen(n, 2 if n == 0 else 1)
             if n == 0:
                 nc.vector.tensor_tensor(lninv[:], lnsig[:], expo_ln[:], ALU.add)
             if n < 5:
@@ -232,60 +244,58 @@ def tile_blp_choice_micro_moments_s13_kernel(
         first_product(1)
 
         nxt = 2
+        qs = (6, 10, 14, 19, 24, 28)
+        q2 = (7, 11, 15, 20, 25, 29, 31)
         for s in range(32):
-            last = s >= 28
-            if not last:
+            if s < 28:
                 add_logs(s)
             elif s == 28:
-                for half in range(2):
+                for lo, hi in fine:
                     for i in range(4):
-                        add_logs(28 + i, slice(256 * half, 256 * (half + 1)))
-                    exponentiate(7, half)
-                    if half == 0:
-                        quant_share(6)
+                        add_logs(28 + i, lo, hi)
+                    exponentiate(7, lo, hi)
+                    if lo == 256:
+                        quant_share(6, 0, JH)
+                        for i in range(4):
+                            second_product(6, i)
             if s + 6 < TILES:
                 widen(s + 6)
             if s % 2 == 1 and (s + 3) // 2 < TILES // 2:
                 quant_tastes((s + 3) // 2)
             if s == 9 or s == 11:
                 quant_chars((s - 9) // 2, 1)
-            if s < 16:
-                if s % 4 == 2 and s >= 6:
-                    quant_share(s // 4 - 1)
-            else:
-                if s % 4 == 2 and s < 28:
-                    quant_share(s // 4 - 1)
-            if last and s == 30:
-                quant_share(7, (0, 1))
-                quant_share(7, (1, 2))
+            if s in qs:
+                quant_share(qs.index(s), 0, JH)
             if s + 5 < TILES:
                 turn(s + 5)
-            if s >= 7:
-                b = (s - 7) // 4
-                second_product(b, (s - 7) % 4)
+            for b in range(6):
+                if 0 <= s - q2[b] < 4 // 4:
+                    for i in range(4):
+                        second_product(b, 4 * (s - q2[b]) + i)
             target = s + 2 if s < 13 else s + 4
             while nxt <= min(target, 31):
                 first_product(nxt)
                 nxt += 1
             if s < 16:
                 if s >= 4 and s % 4 < 2:
-                    exponentiate(s // 4 - 1, s % 4)
+                    exponentiate(s // 4 - 1, 256 * (s % 4), 256 * (s % 4 + 1))
                 if s + 5 < TILES:
                     gather(s + 5)
                 if s in (2, 3, 6, 7):
                     i = (2, 3, 6, 7).index(s)
                     interleave_chars(i // 2, 1, i % 2)
-            if s == 16:
-                exponentiate(3, 0)
-                exponentiate(3, 1)
+            if s == 15:
+                for lo, hi in whole:
+                    exponentiate(3, lo, hi)
             if s > 16 and s % 4 == 3 and s < 28:
-                exponentiate(s // 4, 0)
-                exponentiate(s // 4, 1)
+                for lo, hi in whole:
+                    exponentiate(s // 4, lo, hi)
             if s == 22:
                 for m in range(4):
                     store(0, m, "scalar")
-        for i in range(25, 32):
-            b, m = divmod(i, 4)
-            second_product(b, m)
+        for lo, hi in fine:
+            quant_share(7, lo, hi)
+        for m in range(4):
+            second_product(7, m)
         for m in range(4):
             store(1, m, "scalar" if m % 2 else "vector")

@@ -35,8 +35,8 @@ def tile_blp_choice_micro_moments_s13_kernel(
         psum = ctx.enter_context(tc.psum_pool(name="psum", bufs=1))
         ctx.enter_context(tc.manual_schedule())
 
-        inv_rows = keep.tile([P, 512], BF16, name="inv_rows", align_bytes=64)
-        nc.vector.memset(inv_rows[:], 0.0)
+        rows = keep.tile([P, 256], F32, name="rows", align_bytes=64)
+        nc.vector.memset(rows[:], 0.0)
         one = keep.tile([P, 1], F32, name="one")
         nc.vector.memset(one[:], 1.0)
         ident = keep.tile([P, P], F32, name="ident")
@@ -47,21 +47,19 @@ def tile_blp_choice_micro_moments_s13_kernel(
         t_view = tastes_bytes.rearrange("(g p t) k -> g p t k", p=P, t=4)
         raw = [keep.tile([P, 4, K], U8, name="raw%d" % g, align_bytes=64) for g in range(GROUPS)]
         scale = keep.tile([P, K], F32, name="scale", align_bytes=64)
-        scale_row = tastes_scale.rearrange("o k -> (o k)")
         c_view = chars.rearrange("(g p t) j -> g p t j", p=P, t=4)
         craw = [[keep.tile([P, 4, JH], BF16, name="craw%d%d" % (g, h), align_bytes=64) for h in range(2)] for g in range(2)]
         delta_bc = keep.tile([P, J], BF16, name="delta_bc", align_bytes=64)
         dwords = keep.tile([P, GROUPS, 2 * M], U8, name="dwords", align_bytes=64)
 
-        nc.scalar.dma_start(out=scale[:, 0:512], in_=scale_row[0:512].partition_broadcast(P))
+        nc.sync.dma_start(out=rows[0:8, 0:P], in_=tastes_scale.rearrange("o (m n) -> (o m) n", n=P))
+        nc.scalar.dma_start(out=rows[8:12, 0:P].bitcast(BF16), in_=delta.rearrange("(m n) -> m n", n=2 * P))
+        nc.scalar.dma_start(out=rows[12:16, :].bitcast(BF16), in_=inv_denom.rearrange("(g r) -> g r", g=GROUPS))
         nc.sync.dma_start(out=raw[0][:, 0:1, :], in_=t_view[0][:, 0:1, :])
-        nc.sync.dma_start(out=inv_rows[0:GROUPS, :], in_=inv_denom.rearrange("(g r) -> g r", g=GROUPS))
-        nc.sync.dma_start(out=scale[:, 512:1024], in_=scale_row[512:1024].partition_broadcast(P))
-        nc.sync.dma_start(out=raw[0][:, 1:4, :], in_=t_view[0][:, 1:4, :])
         nc.sync.dma_start(out=craw[0][0][:], in_=c_view[0][:, :, 0:JH])
+        nc.sync.dma_start(out=raw[0][:, 1:4, :], in_=t_view[0][:, 1:4, :])
         nc.sync.dma_start(out=craw[1][0][:], in_=c_view[1][:, :, 0:JH])
         nc.sync.dma_start(out=raw[1][:], in_=t_view[1])
-        nc.sync.dma_start(out=delta_bc[:], in_=delta.partition_broadcast(P))
         nc.sync.dma_start(out=craw[0][1][:], in_=c_view[0][:, :, JH:J])
         nc.sync.dma_start(out=craw[1][1][:], in_=c_view[1][:, :, JH:J])
         nc.sync.dma_start(out=raw[2][:], in_=t_view[2])
@@ -78,13 +76,21 @@ def tile_blp_choice_micro_moments_s13_kernel(
 
         scrap = keep.tile([P, 1], F32, name="scrap")
         nc.scalar.activation(scrap[:], one[:], ACT.Ln)
+        cols_t = psum.tile([P, P], F32, name="cols_t", tag="acc0", bufs=1)
+        nc.tensor.transpose(cols_t[:], rows[:, 0:P], ident[:])
         inv_t = psum.tile([P, 2, P], F32, name="inv_t", tag="mu", bufs=2)
         for u in range(2):
-            nc.tensor.transpose(inv_t[:, u, :], inv_rows[:].bitcast(F32)[:, u:256:2], ident[:])
+            nc.tensor.transpose(inv_t[:, u, :], rows[:, u:256:2], ident[:])
+        cols = keep.tile([P, 12], F32, name="cols")
+        nc.vector.tensor_copy(out=cols[:], in_=cols_t[:, 0:12])
+        spread = [psum.tile([P, 4, P], F32, name="spread%d" % i, tag="acc%d" % (i + 1), bufs=1) for i in range(3)]
+        for i in range(3):
+            for m in range(4):
+                nc.tensor.transpose(spread[i][:, m, :], cols[:, 4 * i + m : 4 * i + m + 1].to_broadcast([P, P]), ident[:])
         inv32 = keep.tile([P, TILES], F32, name="inv32")
         nc.vector.tensor_copy(
             out=inv32[:].rearrange("p (g u e) -> p u g e", u=2, e=2),
-            in_=inv_t[:, :, 0:GROUPS].bitcast(BF16).rearrange("p u (g e) -> p u g e", e=2),
+            in_=inv_t[:, :, 12:16].bitcast(BF16).rearrange("p u (g e) -> p u g e", e=2),
         )
         expo = keep.tile([P, TILES], I32, name="expo")
         sig = keep.tile([P, TILES], I32, name="sig")
@@ -92,10 +98,11 @@ def tile_blp_choice_micro_moments_s13_kernel(
         nc.vector.tensor_scalar(expo[:], inv32[:].bitcast(I32), 23, None, ALU.logical_shift_right)
         lnsig = keep.tile([P, TILES], F32, name="lnsig")
         nc.scalar.activation(lnsig[:], sig[:].bitcast(F32), ACT.Ln)
-        nc.scalar.activation(scrap[:], one[:], ACT.Exp)
         expo_ln = keep.tile([P, TILES], F32, name="expo_ln")
         nc.vector.tensor_scalar(expo_ln[:], expo[:], -127.0, LN2, ALU.add, ALU.mult)
         lninv = keep.tile([P, TILES], F32, name="lninv")
+        nc.vector.tensor_copy(out=scale[:, 0:512], in_=spread[0][:].rearrange("p m n -> p (m n)"))
+        nc.scalar.copy(out=scale[:, 512:1024], in_=spread[1][:].rearrange("p m n -> p (m n)"))
 
         wid = {}
         xts = {}
@@ -225,21 +232,27 @@ def tile_blp_choice_micro_moments_s13_kernel(
                 nc.vector.tensor_copy(out=res[:], in_=accs[h, m][:])
             nc.sync.dma_start(out=out[P * m : P * (m + 1), h * JH : (h + 1) * JH], in_=res[:])
 
+        interleave_chars(0, 0, 0)
+        interleave_chars(0, 0, 1)
         for n in range(6):
+            if n == 3:
+                quant_chars(0, 0)
             if n == 4:
                 quant_tastes(0)
-            if n == 5:
-                quant_chars(0, 0)
-                quant_tastes(1)
             widen(n, 2 if n == 0 else 1)
             if n == 0:
                 nc.vector.tensor_tensor(lninv[:], lnsig[:], expo_ln[:], ALU.add)
             if n < 5:
                 turn(n)
                 gather(n)
-            if n < 4:
-                interleave_chars(n // 2, 0, n % 2)
-        quant_chars(1, 0)
+            if n in (1, 2):
+                interleave_chars(1, 0, n - 1)
+            if n == 3:
+                nc.scalar.copy(out=delta_bc[:].bitcast(F32), in_=spread[2][:].rearrange("p m n -> p (m n)"))
+            if n == 4:
+                quant_chars(1, 0)
+        nc.scalar.activation(scrap[:], one[:], ACT.Exp)
+        quant_tastes(1)
         first_product(0)
         first_product(1)
 

@@ -24,6 +24,19 @@ TILES = C // P
 JH = 512
 LN2 = math.log(2.0)
 
+WIDEN_AT = (0, 0, 1, 2, 5, 5, 6, 6, 8, 8)
+TURN_AT = (0, 1, 2, 3, 4, 5, 5, 8, 9, 9, 9)
+QUANT_TASTES_AT = (1, 3, 5, 7, 10, 12)
+CI_AT = (4, 1, 1, 10)
+QUANT_CHARS_AT = (13, 13)
+EXP_AT = ((5, 6), (8, 8), (14, 15), (18, 18), (19, 22), (24, 24), (27, 28), (29, 29, 30))
+QUANT_SHARE_AT = ((7,), (10,), (17,), (20,), (27,), (27,), (29,), (30, 31, 31))
+SECOND_AT = ((8, 8, 8, 9), (11, 11, 12, 13), (18, 18, 18, 18), (20, 20, 20, 20), (28, 28, 28, 28), (28, 28, 28, 29), (30, 30, 30, 31), (31, 31, 31, 31))
+EVAC_AT = (23, 22, 22, 23)
+EVAC_ON = "VSSV"
+AHEAD = (2, 17, 4)
+FINE = ((0, 256), (256, 384), (384, 512))
+
 
 def tile_blp_choice_micro_moments_s13_kernel(
     tc, tastes_bytes, tastes_scale, chars, delta, inv_denom, demo_words, demo_scales, out
@@ -35,10 +48,12 @@ def tile_blp_choice_micro_moments_s13_kernel(
         psum = ctx.enter_context(tc.psum_pool(name="psum", bufs=1))
         ctx.enter_context(tc.manual_schedule())
 
-        rows = keep.tile([P, 256], F32, name="rows", align_bytes=64)
-        nc.vector.memset(rows[:], 0.0)
         one = keep.tile([P, 1], F32, name="one")
         nc.vector.memset(one[:], 1.0)
+        inv_rows = keep.tile([P, 256], F32, name="inv_rows", align_bytes=64)
+        nc.vector.memset(inv_rows[:], 0.0)
+        scale_cols = keep.tile([P, 2, 4], F32, name="scale_cols")
+        delta_cols = keep.tile([P, 4], F32, name="delta_cols")
         ident = keep.tile([P, P], F32, name="ident")
         make_identity(nc, ident[:])
         dscale = keep.tile([P, GROUPS, M], U8, name="dscale", align_bytes=64)
@@ -52,10 +67,10 @@ def tile_blp_choice_micro_moments_s13_kernel(
         delta_bc = keep.tile([P, J], BF16, name="delta_bc", align_bytes=64)
         dwords = keep.tile([P, GROUPS, 2 * M], U8, name="dwords", align_bytes=64)
 
-        nc.sync.dma_start(out=rows[0:8, 0:P], in_=tastes_scale.rearrange("o (m n) -> (o m) n", n=P))
-        nc.scalar.dma_start(out=rows[8:12, 0:P].bitcast(BF16), in_=delta.rearrange("(m n) -> m n", n=2 * P))
-        nc.scalar.dma_start(out=rows[12:16, :].bitcast(BF16), in_=inv_denom.rearrange("(g r) -> g r", g=GROUPS))
+        nc.sync.dma_start(out=scale_cols[:], in_=tastes_scale.rearrange("o (h n i) -> (o n) h i", h=2, i=4))
         nc.sync.dma_start(out=raw[0][:, 0:1, :], in_=t_view[0][:, 0:1, :])
+        nc.sync.dma_start(out=inv_rows[0:GROUPS, :].bitcast(BF16), in_=inv_denom.rearrange("(g r) -> g r", g=GROUPS))
+        nc.sync.dma_start(out=delta_cols[:].bitcast(BF16), in_=delta.rearrange("(n i) -> n i", i=8))
         nc.sync.dma_start(out=craw[0][0][:], in_=c_view[0][:, :, 0:JH])
         nc.sync.dma_start(out=raw[0][:, 1:4, :], in_=t_view[0][:, 1:4, :])
         nc.sync.dma_start(out=craw[1][0][:], in_=c_view[1][:, :, 0:JH])
@@ -76,33 +91,47 @@ def tile_blp_choice_micro_moments_s13_kernel(
 
         scrap = keep.tile([P, 1], F32, name="scrap")
         nc.scalar.activation(scrap[:], one[:], ACT.Ln)
-        cols_t = psum.tile([P, P], F32, name="cols_t", tag="acc0", bufs=1)
-        nc.tensor.transpose(cols_t[:], rows[:, 0:P], ident[:])
-        inv_t = psum.tile([P, 2, P], F32, name="inv_t", tag="mu", bufs=2)
-        for u in range(2):
-            nc.tensor.transpose(inv_t[:, u, :], rows[:, u:256:2], ident[:])
-        cols = keep.tile([P, 12], F32, name="cols")
-        nc.vector.tensor_copy(out=cols[:], in_=cols_t[:, 0:12])
-        spread = [psum.tile([P, 4, P], F32, name="spread%d" % i, tag="acc%d" % (i + 1), bufs=1) for i in range(3)]
-        for i in range(3):
-            for m in range(4):
-                nc.tensor.transpose(spread[i][:, m, :], cols[:, 4 * i + m : 4 * i + m + 1].to_broadcast([P, P]), ident[:])
+        def spread(columns, tag):
+            x = psum.tile([P, 4, P], F32, name="spread", tag=tag, bufs=1)
+            for i in range(4):
+                nc.tensor.transpose(x[:, i, :], columns[:, i : i + 1].to_broadcast([P, P]), ident[:])
+            return x[:].rearrange("p i n -> p n i")
+
+        scale_spread = [spread(scale_cols[:, h, :], "acc%d" % h) for h in range(2)]
+        nc.vector.tensor_copy(out=scale[:, 0:512].rearrange("p (n i) -> p n i", i=4), in_=scale_spread[0])
+        nc.scalar.copy(out=scale[:, 512:1024].rearrange("p (n i) -> p n i", i=4), in_=scale_spread[1])
+
         inv32 = keep.tile([P, TILES], F32, name="inv32")
-        nc.vector.tensor_copy(
-            out=inv32[:].rearrange("p (g u e) -> p u g e", u=2, e=2),
-            in_=inv_t[:, :, 12:16].bitcast(BF16).rearrange("p u (g e) -> p u g e", e=2),
-        )
         expo = keep.tile([P, TILES], I32, name="expo")
         sig = keep.tile([P, TILES], I32, name="sig")
-        nc.vector.tensor_scalar(sig[:], inv32[:].bitcast(I32), 0x7FFFFF, 0x3F800000, ALU.bitwise_and, ALU.bitwise_or)
-        nc.vector.tensor_scalar(expo[:], inv32[:].bitcast(I32), 23, None, ALU.logical_shift_right)
         lnsig = keep.tile([P, TILES], F32, name="lnsig")
-        nc.scalar.activation(lnsig[:], sig[:].bitcast(F32), ACT.Ln)
         expo_ln = keep.tile([P, TILES], F32, name="expo_ln")
-        nc.vector.tensor_scalar(expo_ln[:], expo[:], -127.0, LN2, ALU.add, ALU.mult)
         lninv = keep.tile([P, TILES], F32, name="lninv")
-        nc.vector.tensor_copy(out=scale[:, 0:512], in_=spread[0][:].rearrange("p m n -> p (m n)"))
-        nc.scalar.copy(out=scale[:, 512:1024], in_=spread[1][:].rearrange("p m n -> p (m n)"))
+
+        inv_t = psum.tile([P, 2, P], F32, name="inv_t", tag="acc3", bufs=1)
+        for u in range(2):
+            nc.tensor.transpose(inv_t[:, u, :], inv_rows[:, u:256:2], ident[:])
+        delta_spread = spread(delta_cols[:], "acc2")
+
+        def turn_weights():
+            nc.vector.tensor_copy(
+                out=inv32[:].rearrange("p (g u e) -> p u g e", u=2, e=2),
+                in_=inv_t[:, :, 0:GROUPS].bitcast(BF16).rearrange("p u (g e) -> p u g e", e=2),
+            )
+
+        def split_weights():
+            nc.vector.tensor_scalar(sig[:], inv32[:].bitcast(I32), 0x7FFFFF, 0x3F800000, ALU.bitwise_and, ALU.bitwise_or)
+            nc.vector.tensor_scalar(expo[:], inv32[:].bitcast(I32), 23, None, ALU.logical_shift_right)
+            nc.scalar.activation(lnsig[:], sig[:].bitcast(F32), ACT.Ln)
+
+        def scale_exponents():
+            nc.vector.tensor_scalar(expo_ln[:], expo[:], -127.0, LN2, ALU.add, ALU.mult)
+
+        def join_logs():
+            nc.vector.tensor_tensor(lninv[:], lnsig[:], expo_ln[:], ALU.add)
+
+        def spread_delta():
+            nc.scalar.copy(out=delta_bc[:].bitcast(F32).rearrange("p (n i) -> p n i", i=4), in_=delta_spread)
 
         wid = {}
         xts = {}
@@ -156,8 +185,6 @@ def tile_blp_choice_micro_moments_s13_kernel(
         shares = {}
         scodes = {}
         accs = {}
-        whole = ((0, 256), (256, 512))
-        fine = ((0, 256), (256, 384), (384, 512))
 
         def first_product(s):
             h, n = divmod(s, TILES)
@@ -240,75 +267,73 @@ def tile_blp_choice_micro_moments_s13_kernel(
             if n == 4:
                 quant_tastes(0)
             widen(n, 2 if n == 0 else 1)
-            if n == 0:
-                nc.vector.tensor_tensor(lninv[:], lnsig[:], expo_ln[:], ALU.add)
             if n < 5:
                 turn(n)
                 gather(n)
             if n in (1, 2):
                 interleave_chars(1, 0, n - 1)
+            if n == 0:
+                turn_weights()
+            if n == 1:
+                split_weights()
+            if n == 2:
+                scale_exponents()
+                spread_delta()
             if n == 3:
-                nc.scalar.copy(out=delta_bc[:].bitcast(F32), in_=spread[2][:].rearrange("p m n -> p (m n)"))
+                join_logs()
             if n == 4:
+                nc.scalar.activation(scrap[:], one[:], ACT.Exp)
                 quant_chars(1, 0)
-        nc.scalar.activation(scrap[:], one[:], ACT.Exp)
         quant_tastes(1)
         first_product(0)
         first_product(1)
 
         nxt = 2
-        qs = (6, 10, 14, 19, 24, 28)
-        q2 = (7, 11, 15, 20, 25, 29, 31)
         for s in range(32):
             if s < 28:
                 add_logs(s)
-            elif s == 28:
-                for lo, hi in fine:
-                    for i in range(4):
-                        add_logs(28 + i, lo, hi)
-                    exponentiate(7, lo, hi)
-                    if lo == 256:
-                        quant_share(6, 0, JH)
-                        for i in range(4):
-                            second_product(6, i)
-            if s + 6 < TILES:
-                widen(s + 6)
-            if s % 2 == 1 and (s + 3) // 2 < TILES // 2:
-                quant_tastes((s + 3) // 2)
-            if s == 9 or s == 11:
-                quant_chars((s - 9) // 2, 1)
-            if s in qs:
-                quant_share(qs.index(s), 0, JH)
-            if s + 5 < TILES:
-                turn(s + 5)
-            for b in range(6):
-                if 0 <= s - q2[b] < 4 // 4:
-                    for i in range(4):
-                        second_product(b, 4 * (s - q2[b]) + i)
-            target = s + 2 if s < 13 else s + 4
+            elif s < 28 + len(FINE):
+                lo, hi = FINE[s - 28]
+                for i in range(4):
+                    add_logs(28 + i, lo, hi)
+            for i in range(10):
+                if WIDEN_AT[i] == s:
+                    widen(6 + i)
+            for i in range(6):
+                if QUANT_TASTES_AT[i] == s:
+                    quant_tastes(2 + i)
+            for g in range(2):
+                if QUANT_CHARS_AT[g] == s:
+                    quant_chars(g, 1)
+            for b in range(8):
+                for i in range(len(QUANT_SHARE_AT[b])):
+                    if QUANT_SHARE_AT[b][i] == s:
+                        lo, hi = FINE[i] if b == 7 else (0, JH)
+                        quant_share(b, lo, hi)
+            for i in range(11):
+                if TURN_AT[i] == s:
+                    turn(5 + i)
+            for b in range(8):
+                for m in range(4):
+                    if SECOND_AT[b][m] == s:
+                        second_product(b, m)
+            target = s + AHEAD[0] if s < AHEAD[1] else s + AHEAD[2]
             while nxt <= min(target, 31):
                 first_product(nxt)
                 nxt += 1
-            if s < 16:
-                if s >= 4 and s % 4 < 2:
-                    exponentiate(s // 4 - 1, 256 * (s % 4), 256 * (s % 4 + 1))
-                if s + 5 < TILES:
-                    gather(s + 5)
-                if s in (2, 3, 6, 7):
-                    i = (2, 3, 6, 7).index(s)
+            for b in range(8):
+                for i in range(len(EXP_AT[b])):
+                    if EXP_AT[b][i] == s:
+                        lo, hi = FINE[i] if b == 7 else (256 * i, 256 * (i + 1))
+                        exponentiate(b, lo, hi)
+            for i in range(11):
+                if TURN_AT[i] == s:
+                    gather(5 + i)
+            for i in range(4):
+                if CI_AT[i] == s:
                     interleave_chars(i // 2, 1, i % 2)
-            if s == 15:
-                for lo, hi in whole:
-                    exponentiate(3, lo, hi)
-            if s > 16 and s % 4 == 3 and s < 28:
-                for lo, hi in whole:
-                    exponentiate(s // 4, lo, hi)
-            if s == 22:
-                for m in range(4):
-                    store(0, m, "scalar")
-        for lo, hi in fine:
-            quant_share(7, lo, hi)
-        for m in range(4):
-            second_product(7, m)
+            for m in range(4):
+                if EVAC_AT[m] == s:
+                    store(0, m, "scalar" if EVAC_ON[m] == "S" else "vector")
         for m in range(4):
             store(1, m, "scalar" if m % 2 else "vector")

@@ -19,23 +19,36 @@ ALU = mybir.AluOpType
 ACT = mybir.ActivationFunctionType
 
 P = 128
-GROUPS = C // 512
+PACK = 4
+PASS = P * PACK
+HALF = 512
+HALVES = J // HALF
+GROUPS = C // PASS
 TILES = C // P
-JH = 512
+K_PASSES = K // PASS
+M_TILES = M // P
+UNITS = HALVES * TILES
 LN2 = math.log(2.0)
 
-WIDEN_AT = (0, 0, 1, 2, 5, 5, 6, 6, 8, 8)
-TURN_AT = (0, 1, 2, 3, 4, 5, 5, 8, 9, 9, 9)
-QUANT_TASTES_AT = (1, 3, 5, 7, 10, 12)
-CI_AT = (4, 1, 1, 10)
-QUANT_CHARS_AT = (13, 13)
-EXP_AT = ((5, 6), (8, 8), (14, 15), (18, 18), (19, 22), (24, 24), (27, 28), (29, 29, 30))
-QUANT_SHARE_AT = ((7,), (10,), (17,), (20,), (27,), (27,), (29,), (30, 31, 31))
-SECOND_AT = ((8, 8, 8, 9), (11, 11, 12, 13), (18, 18, 18, 18), (20, 20, 20, 20), (28, 28, 28, 28), (28, 28, 28, 29), (30, 30, 30, 31), (31, 31, 31, 31))
-EVAC_AT = (23, 22, 22, 23)
-EVAC_ON = "VSSV"
-AHEAD = (2, 17, 4)
-FINE = ((0, 256), (256, 384), (384, 512))
+PIECES = ((0, 256), (256, 384), (384, HALF))
+FIRST_PIECE = UNITS - 4
+CYCLES = UNITS
+LAST = HALVES * GROUPS - 1
+
+HEAD_TILES = 6
+LATE_TILE = 14
+
+EXP_CYCLE = (5, 9, 13, 17, 20, 24, 28)
+QUANT_CYCLE = (7, 11, 17, 19, 27, 27, 29)
+LAST_EXP_CYCLE = (28, 29, 30)
+LAST_QUANT_CYCLE = (30, 31, 31)
+CHARS_COPY_CYCLE = (0, 1, 2, 3)
+CHARS_QUANT_CYCLE = 13
+STORE_CYCLE = (22, 22, 23, 23)
+
+
+def late(n):
+    return 1 if n >= LATE_TILE else 0
 
 
 def tile_blp_choice_micro_moments_s13_kernel(
@@ -48,239 +61,247 @@ def tile_blp_choice_micro_moments_s13_kernel(
         psum = ctx.enter_context(tc.psum_pool(name="psum", bufs=1))
         ctx.enter_context(tc.manual_schedule())
 
+
         one = keep.tile([P, 1], F32, name="one")
         nc.vector.memset(one[:], 1.0)
-        inv_rows = keep.tile([P, 256], F32, name="inv_rows", align_bytes=64)
+        inv_rows = keep.tile([P, PASS // 2], F32, name="inv_rows", align_bytes=64)
         nc.vector.memset(inv_rows[:], 0.0)
-        scale_cols = keep.tile([P, 2, 4], F32, name="scale_cols")
-        delta_cols = keep.tile([P, 4], F32, name="delta_cols")
+        scale_cols = keep.tile([P, K_PASSES, PACK], F32, name="scale_cols")
+        delta_cols = keep.tile([P, PACK], F32, name="delta_cols")
         ident = keep.tile([P, P], F32, name="ident")
         make_identity(nc, ident[:])
-        dscale = keep.tile([P, GROUPS, M], U8, name="dscale", align_bytes=64)
-        nc.gpsimd.memset(dscale[:].rearrange("p g m -> p (g m)").bitcast(I32), 0)
+        demo_planes = keep.tile([P, GROUPS, M], U8, name="demo_planes", align_bytes=64)
+        nc.gpsimd.memset(demo_planes[:].rearrange("p g m -> p (g m)").bitcast(I32), 0)
 
-        t_view = tastes_bytes.rearrange("(g p t) k -> g p t k", p=P, t=4)
-        raw = [keep.tile([P, 4, K], U8, name="raw%d" % g, align_bytes=64) for g in range(GROUPS)]
-        scale = keep.tile([P, K], F32, name="scale", align_bytes=64)
-        c_view = chars.rearrange("(g p t) j -> g p t j", p=P, t=4)
-        craw = [[keep.tile([P, 4, JH], BF16, name="craw%d%d" % (g, h), align_bytes=64) for h in range(2)] for g in range(2)]
-        delta_bc = keep.tile([P, J], BF16, name="delta_bc", align_bytes=64)
-        dwords = keep.tile([P, GROUPS, 2 * M], U8, name="dwords", align_bytes=64)
+        tastes_view = tastes_bytes.rearrange("(g p t) k -> g p t k", p=P, t=PACK)
+        chars_view = chars.rearrange("(g p t) j -> g p t j", p=P, t=PACK)
+        tastes_raw = [keep.tile([P, PACK, K], U8, name="tastes_raw%d" % g, align_bytes=64) for g in range(GROUPS)]
+        chars_raw = [
+            [keep.tile([P, PACK, HALF], BF16, name="chars_raw%d%d" % (g, h), align_bytes=64) for h in range(HALVES)]
+            for g in range(K_PASSES)
+        ]
+        demo_codes = keep.tile([P, GROUPS, 2 * M], U8, name="demo_codes", align_bytes=64)
 
-        nc.sync.dma_start(out=scale_cols[:], in_=tastes_scale.rearrange("o (h n i) -> (o n) h i", h=2, i=4))
-        nc.sync.dma_start(out=raw[0][:, 0:1, :], in_=t_view[0][:, 0:1, :])
+        nc.sync.dma_start(out=scale_cols[:], in_=tastes_scale.rearrange("o (h n i) -> (o n) h i", h=K_PASSES, i=PACK))
+        nc.sync.dma_start(out=tastes_raw[0][:, 0:1, :], in_=tastes_view[0][:, 0:1, :])
         nc.sync.dma_start(out=inv_rows[0:GROUPS, :].bitcast(BF16), in_=inv_denom.rearrange("(g r) -> g r", g=GROUPS))
-        nc.sync.dma_start(out=delta_cols[:].bitcast(BF16), in_=delta.rearrange("(n i) -> n i", i=8))
-        nc.sync.dma_start(out=craw[0][0][:], in_=c_view[0][:, :, 0:JH])
-        nc.sync.dma_start(out=raw[0][:, 1:4, :], in_=t_view[0][:, 1:4, :])
-        nc.sync.dma_start(out=craw[1][0][:], in_=c_view[1][:, :, 0:JH])
-        nc.sync.dma_start(out=raw[1][:], in_=t_view[1])
-        nc.sync.dma_start(out=craw[0][1][:], in_=c_view[0][:, :, JH:J])
-        nc.sync.dma_start(out=craw[1][1][:], in_=c_view[1][:, :, JH:J])
-        nc.sync.dma_start(out=raw[2][:], in_=t_view[2])
-        nc.sync.dma_start(out=raw[3][:], in_=t_view[3])
+        nc.sync.dma_start(out=delta_cols[:].bitcast(BF16), in_=delta.rearrange("(n i) -> n i", i=2 * PACK))
+        nc.sync.dma_start(out=chars_raw[0][0][:], in_=chars_view[0][:, :, 0:HALF])
+        nc.sync.dma_start(out=tastes_raw[0][:, 1:PACK, :], in_=tastes_view[0][:, 1:PACK, :])
+        nc.sync.dma_start(out=chars_raw[1][0][:], in_=chars_view[1][:, :, 0:HALF])
+        nc.sync.dma_start(out=tastes_raw[1][:], in_=tastes_view[1])
+        nc.sync.dma_start(out=chars_raw[0][1][:], in_=chars_view[0][:, :, HALF:J])
+        nc.sync.dma_start(out=chars_raw[1][1][:], in_=chars_view[1][:, :, HALF:J])
+        nc.sync.dma_start(out=tastes_raw[2][:], in_=tastes_view[2])
+        nc.sync.dma_start(out=tastes_raw[3][:], in_=tastes_view[3])
         nc.sync.dma_start(
-            out=dwords[:].rearrange("p g n -> p (g n)").bitcast(I32).rearrange("p (g n) -> p g n", g=GROUPS),
+            out=demo_codes[:].rearrange("p g n -> p (g n)").bitcast(I32).rearrange("p (g n) -> p g n", g=GROUPS),
             in_=demo_words.bitcast(I32).rearrange("g p n -> p g n"),
         )
         for q in range(4):
             nc.sync.dma_start(
-                out=dscale[32 * q : 32 * q + 4, :, :].rearrange("p g m -> p (g m)").bitcast(I32).rearrange("p (g m) -> p g m", g=GROUPS),
+                out=demo_planes[32 * q : 32 * q + 4, :, :]
+                .rearrange("p g m -> p (g m)")
+                .bitcast(I32)
+                .rearrange("p (g m) -> p g m", g=GROUPS),
                 in_=demo_scales.bitcast(I32).rearrange("g q m -> q g m")[4 * q : 4 * q + 4, :, :],
             )
 
-        scrap = keep.tile([P, 1], F32, name="scrap")
-        nc.scalar.activation(scrap[:], one[:], ACT.Ln)
         def spread(columns, tag):
-            x = psum.tile([P, 4, P], F32, name="spread", tag=tag, bufs=1)
-            for i in range(4):
+            x = psum.tile([P, PACK, P], F32, name="spread", tag=tag, bufs=1)
+            for i in range(PACK):
                 nc.tensor.transpose(x[:, i, :], columns[:, i : i + 1].to_broadcast([P, P]), ident[:])
             return x[:].rearrange("p i n -> p n i")
 
-        scale_spread = [spread(scale_cols[:, h, :], "acc%d" % h) for h in range(2)]
-        nc.vector.tensor_copy(out=scale[:, 0:512].rearrange("p (n i) -> p n i", i=4), in_=scale_spread[0])
-        nc.scalar.copy(out=scale[:, 512:1024].rearrange("p (n i) -> p n i", i=4), in_=scale_spread[1])
+        scrap = keep.tile([P, 1], F32, name="scrap")
+        nc.scalar.activation(scrap[:], one[:], ACT.Ln)
 
-        inv32 = keep.tile([P, TILES], F32, name="inv32")
-        expo = keep.tile([P, TILES], I32, name="expo")
-        sig = keep.tile([P, TILES], I32, name="sig")
-        lnsig = keep.tile([P, TILES], F32, name="lnsig")
-        expo_ln = keep.tile([P, TILES], F32, name="expo_ln")
-        lninv = keep.tile([P, TILES], F32, name="lninv")
+        scale = keep.tile([P, K], F32, name="scale", align_bytes=64)
+        scale_rows = [spread(scale_cols[:, g, :], "acc%d" % g) for g in range(K_PASSES)]
+        nc.vector.tensor_copy(out=scale[:, 0:PASS].rearrange("p (n i) -> p n i", i=PACK), in_=scale_rows[0])
+        nc.scalar.copy(out=scale[:, PASS:K].rearrange("p (n i) -> p n i", i=PACK), in_=scale_rows[1])
 
         inv_t = psum.tile([P, 2, P], F32, name="inv_t", tag="acc3", bufs=1)
         for u in range(2):
-            nc.tensor.transpose(inv_t[:, u, :], inv_rows[:, u:256:2], ident[:])
-        delta_spread = spread(delta_cols[:], "acc2")
+            nc.tensor.transpose(inv_t[:, u, :], inv_rows[:, u : PASS // 2 : 2], ident[:])
 
-        def turn_weights():
+        delta_rows = spread(delta_cols[:], "acc2")
+        delta_all = keep.tile([P, J], BF16, name="delta_all", align_bytes=64)
+
+        inv = keep.tile([P, TILES], F32, name="inv")
+        exponent = keep.tile([P, TILES], I32, name="exponent")
+        significand = keep.tile([P, TILES], I32, name="significand")
+        ln_significand = keep.tile([P, TILES], F32, name="ln_significand")
+        ln_exponent = keep.tile([P, TILES], F32, name="ln_exponent")
+        ln_inv = keep.tile([P, TILES], F32, name="ln_inv")
+
+        def take_inv():
             nc.vector.tensor_copy(
-                out=inv32[:].rearrange("p (g u e) -> p u g e", u=2, e=2),
+                out=inv[:].rearrange("p (g u e) -> p u g e", u=2, e=2),
                 in_=inv_t[:, :, 0:GROUPS].bitcast(BF16).rearrange("p u (g e) -> p u g e", e=2),
             )
 
-        def split_weights():
-            nc.vector.tensor_scalar(sig[:], inv32[:].bitcast(I32), 0x7FFFFF, 0x3F800000, ALU.bitwise_and, ALU.bitwise_or)
-            nc.vector.tensor_scalar(expo[:], inv32[:].bitcast(I32), 23, None, ALU.logical_shift_right)
-            nc.scalar.activation(lnsig[:], sig[:].bitcast(F32), ACT.Ln)
+        def split_inv():
+            bits = inv[:].bitcast(I32)
+            nc.vector.tensor_scalar(significand[:], bits, 0x7FFFFF, 0x3F800000, ALU.bitwise_and, ALU.bitwise_or)
+            nc.vector.tensor_scalar(exponent[:], bits, 23, None, ALU.logical_shift_right)
+            nc.scalar.activation(ln_significand[:], significand[:].bitcast(F32), ACT.Ln)
 
-        def scale_exponents():
-            nc.vector.tensor_scalar(expo_ln[:], expo[:], -127.0, LN2, ALU.add, ALU.mult)
+        def scale_exponent():
+            nc.vector.tensor_scalar(ln_exponent[:], exponent[:], -127.0, LN2, ALU.add, ALU.mult)
 
-        def join_logs():
-            nc.vector.tensor_tensor(lninv[:], lnsig[:], expo_ln[:], ALU.add)
+        def join_ln():
+            nc.vector.tensor_tensor(ln_inv[:], ln_significand[:], ln_exponent[:], ALU.add)
 
-        def spread_delta():
-            nc.scalar.copy(out=delta_bc[:].bitcast(F32).rearrange("p (n i) -> p n i", i=4), in_=delta_spread)
+        widened, turned, pairs = {}, {}, {}
+        tastes_codes = [keep.tile([P, 2 * K // PACK], U32, name="tastes_codes%d" % q, align_bytes=64) for q in range(TILES // 2)]
+        tastes_planes = [keep.tile([P, 2 * K // PACK], U8, name="tastes_planes%d" % q, align_bytes=64) for q in range(TILES // 2)]
 
-        wid = {}
-        xts = {}
-        pairs = {}
-        tcodes = [keep.tile([P, 2 * 256], U32, name="tcodes%d" % q, align_bytes=64) for q in range(TILES // 2)]
-        tscales = [keep.tile([P, 2 * 256], U8, name="tscales%d" % q, align_bytes=64) for q in range(TILES // 2)]
-        cgrp = [[keep.tile([P, JH, 4], BF16, name="cgrp%d%d" % (g, h), align_bytes=64) for h in range(2)] for g in range(2)]
-        ccodes = [[keep.tile([P, JH], U32, name="ccodes%d%d" % (g, h), align_bytes=64) for h in range(2)] for g in range(2)]
-        cscales = [[keep.tile([P, JH], U8, name="cscales%d%d" % (g, h), align_bytes=64) for h in range(2)] for g in range(2)]
-
-        def widen(n, pieces=1):
-            w = ring.tile([P, K], BF16, name="wid", tag="wid", bufs=4, align_bytes=64)
-            step = K // pieces
-            for i in range(pieces):
-                cols = slice(step * i, step * (i + 1))
-                nc.vector.tensor_tensor(w[:, cols], raw[n // 4][:, n % 4, cols].bitcast(E4M3), scale[:, cols], ALU.mult)
-            wid[n] = w
+        def widen(n, parts=1):
+            w = ring.tile([P, K], BF16, name="widened", tag="widened", bufs=4, align_bytes=64)
+            for i in range(parts):
+                cols = slice(K // parts * i, K // parts * (i + 1))
+                nc.vector.tensor_tensor(w[:, cols], tastes_raw[n // 4][:, n % 4, cols].bitcast(E4M3), scale[:, cols], ALU.mult)
+            widened[n] = w
 
         def turn(n):
-            x = psum.tile([P, 2, 2, P], F32, name="xt", tag="xt", bufs=2)
-            words = wid[n][:].bitcast(F32)
-            for g in range(2):
+            x = psum.tile([P, K_PASSES, 2, P], F32, name="turned", tag="xt", bufs=2)
+            words = widened[n][:].bitcast(F32)
+            for g in range(K_PASSES):
                 for u in range(2):
-                    nc.tensor.transpose(x[:, g, u, :], words[:, 256 * g + u : 256 * (g + 1) : 2], ident[:])
-            xts[n] = x
+                    nc.tensor.transpose(x[:, g, u, :], words[:, PASS // 2 * g + u : PASS // 2 * (g + 1) : 2], ident[:])
+            turned[n] = x
 
-        def gather(n):
+        def take_turned(n):
             q, e = divmod(n, 2)
             if e == 0:
                 pairs[q] = ring.tile([P, 2 * K], BF16, name="pair", tag="pair", bufs=3, align_bytes=64)
-            dst = pairs[q][:, e * K : (e + 1) * K].bitcast(F32).rearrange("p (g r u) -> p g r u", g=2, u=2)
-            nc.scalar.copy(out=dst, in_=xts[n][:].rearrange("p g u r -> p g r u"))
+            dst = pairs[q][:, e * K : (e + 1) * K].bitcast(F32).rearrange("p (g r u) -> p g r u", g=K_PASSES, u=2)
+            nc.scalar.copy(out=dst, in_=turned[n][:].rearrange("p g u r -> p g r u"))
 
         def quant_tastes(q):
-            nc.vector.quantize_mx(out=tcodes[q][:].bitcast(E4M3X4), scales=tscales[q][:], in_=pairs[q][:])
+            nc.vector.quantize_mx(out=tastes_codes[q][:].bitcast(E4M3X4), scales=tastes_planes[q][:], in_=pairs[q][:])
 
-        def interleave_chars(g, h, half):
-            cols = slice(256 * half, 256 * (half + 1))
-            nc.scalar.copy(
-                out=cgrp[g][h][:, cols, :].rearrange("p (c i) t -> p c t i", i=4),
-                in_=craw[g][h][:, :, cols].rearrange("p t (c i) -> p c t i", i=4),
-            )
+        def per_chars(name, shape, dtype):
+            return [
+                [keep.tile(shape, dtype, name="%s%d%d" % (name, g, h), align_bytes=64) for h in range(HALVES)]
+                for g in range(K_PASSES)
+            ]
+
+        chars_grouped = per_chars("chars_grouped", [P, HALF, PACK], BF16)
+        chars_codes = per_chars("chars_codes", [P, HALF], U32)
+        chars_planes = per_chars("chars_planes", [P, HALF], U8)
+
+        def interleave(engine_op, dst, src):
+            engine_op(dst.rearrange("p (c i) t -> p c t i", i=4), src.rearrange("p t (c i) -> p c t i", i=4))
+
+        def group_chars(g, h, part):
+            cols = slice(256 * part, 256 * (part + 1))
+            interleave(lambda o, i: nc.scalar.copy(out=o, in_=i), chars_grouped[g][h][:, cols, :], chars_raw[g][h][:, :, cols])
 
         def quant_chars(g, h):
             nc.vector.quantize_mx(
-                out=ccodes[g][h][:].bitcast(E4M3X4), scales=cscales[g][h][:], in_=cgrp[g][h][:].rearrange("p j t -> p (j t)")
+                out=chars_codes[g][h][:].bitcast(E4M3X4),
+                scales=chars_planes[g][h][:],
+                in_=chars_grouped[g][h][:].rearrange("p j t -> p (j t)"),
             )
 
-        mus = {}
-        xs = {}
-        shares = {}
-        scodes = {}
-        accs = {}
+        mu, logs, share, share_mx, acc = {}, {}, {}, {}, {}
 
         def first_product(s):
             h, n = divmod(s, TILES)
-            tag = "mu" if s < 16 or s % 4 >= 2 else "xt"
-            mu = psum.tile([P, JH], F32, name="mu", tag=tag, bufs=2)
+            tag = "xt" if h == 1 and s % 4 < 2 else "mu"
+            mu[s] = psum.tile([P, HALF], F32, name="mu", tag=tag, bufs=2)
             q, e = divmod(n, 2)
-            for g in range(2):
-                cols = slice(256 * e + 128 * g, 256 * e + 128 * (g + 1))
+            for g in range(K_PASSES):
+                cols = slice(K // PACK * e + P * g, K // PACK * e + P * (g + 1))
                 nc.tensor.matmul_mx(
-                    out=mu[:],
-                    lhsT=tcodes[q][:, cols].bitcast(E4M3X4),
-                    lhsT_scale=tscales[q][:, cols],
-                    rhs=ccodes[g][h][:].bitcast(E4M3X4),
-                    rhs_scale=cscales[g][h][:],
+                    out=mu[s][:],
+                    lhsT=tastes_codes[q][:, cols].bitcast(E4M3X4),
+                    lhsT_scale=tastes_planes[q][:, cols],
+                    rhs=chars_codes[g][h][:].bitcast(E4M3X4),
+                    rhs_scale=chars_planes[g][h][:],
                     start=(g == 0),
-                    stop=(g == 1),
+                    stop=(g == K_PASSES - 1),
                 )
-            mus[s] = mu
 
-        def add_logs(s, lo=0, hi=JH):
+        def add_logs(s, lo, hi):
             h, n = divmod(s, TILES)
-            b = s // 4
-            if n % 4 == 0:
-                xs[b, lo] = ring.tile([P, 4, hi - lo], F32, name="xsum", tag="xsum%d" % (hi - lo), bufs=3 if hi - lo == JH else 2, align_bytes=64)
+            b, t = divmod(s, 4)
+            if t == 0:
+                logs[b, lo] = ring.tile(
+                    [P, 4, hi - lo], F32, name="logs", tag="logs%d" % (hi - lo), bufs=3 if hi - lo == HALF else 2, align_bytes=64
+                )
             nc.vector.scalar_tensor_tensor(
-                out=xs[b, lo][:, n % 4, :],
-                in0=mus[s][:, lo:hi],
-                scalar=lninv[:, n : n + 1],
-                in1=delta_bc[:, h * JH + lo : h * JH + hi],
+                out=logs[b, lo][:, t, :],
+                in0=mu[s][:, lo:hi],
+                scalar=ln_inv[:, n : n + 1],
+                in1=delta_all[:, h * HALF + lo : h * HALF + hi],
                 op0=ALU.add,
                 op1=ALU.add,
             )
 
         def exponentiate(b, lo, hi):
             if lo == 0:
-                shares[b] = ring.tile([P, JH, 4], BF16, name="share", tag="share", bufs=3, align_bytes=64)
-            x = xs[b, lo][:] if (b, lo) in xs and b == 7 else xs[b, 0][:, :, lo:hi]
-            nc.scalar.activation(
-                shares[b][:, lo:hi, :].rearrange("p (c i) t -> p c t i", i=4), x.rearrange("p t (c i) -> p c t i", i=4), ACT.Exp
-            )
+                share[b] = ring.tile([P, HALF, PACK], BF16, name="share", tag="share", bufs=3, align_bytes=64)
+            interleave(lambda o, i: nc.scalar.activation(o, i, ACT.Exp), share[b][:, lo:hi, :], logs[b, lo][:])
 
         def quant_share(b, lo, hi):
             if lo == 0:
-                codes = ring.tile([P, JH], U32, name="scodes", tag="scodes", bufs=3, align_bytes=64)
-                planes = ring.tile([P, JH], U8, name="splanes", tag="splanes", bufs=3, align_bytes=64)
-                scodes[b] = (codes, planes)
-            codes, planes = scodes[b]
+                codes = ring.tile([P, HALF], U32, name="share_codes", tag="share_codes", bufs=3, align_bytes=64)
+                planes = ring.tile([P, HALF], U8, name="share_planes", tag="share_planes", bufs=3, align_bytes=64)
+                share_mx[b] = (codes, planes)
+            codes, planes = share_mx[b]
             nc.vector.quantize_mx(
-                out=codes[:, lo:hi].bitcast(E4M3X4), scales=planes[:, lo:hi], in_=shares[b][:, lo:hi, :].rearrange("p j t -> p (j t)")
+                out=codes[:, lo:hi].bitcast(E4M3X4), scales=planes[:, lo:hi], in_=share[b][:, lo:hi, :].rearrange("p j t -> p (j t)")
             )
 
-        def second_product(b, m):
+        def second_product(b):
             h, g = divmod(b, GROUPS)
-            if g == 0:
-                accs[h, m] = psum.tile([P, JH], F32, name="acc%d" % m, tag="acc%d" % m, bufs=1)
-            codes, planes = scodes[b]
-            nc.tensor.matmul_mx(
-                out=accs[h, m][:],
-                lhsT=dwords[:, g, 2 * P * m : 2 * P * (m + 1)].bitcast(E2M1X4),
-                lhsT_scale=dscale[:, g, P * m : P * (m + 1)],
-                rhs=codes[:].bitcast(E4M3X4),
-                rhs_scale=planes[:],
-                start=(g == 0),
-                stop=(g == GROUPS - 1),
-            )
+            codes, planes = share_mx[b]
+            for m in range(M_TILES):
+                if g == 0:
+                    acc[h, m] = psum.tile([P, HALF], F32, name="acc", tag="acc%d" % m, bufs=1)
+                nc.tensor.matmul_mx(
+                    out=acc[h, m][:],
+                    lhsT=demo_codes[:, g, 2 * P * m : 2 * P * (m + 1)].bitcast(E2M1X4),
+                    lhsT_scale=demo_planes[:, g, P * m : P * (m + 1)],
+                    rhs=codes[:].bitcast(E4M3X4),
+                    rhs_scale=planes[:],
+                    start=(g == 0),
+                    stop=(g == GROUPS - 1),
+                )
 
-        def store(h, m, engine):
-            res = ring.tile([P, JH], F32, name="res", tag="res", bufs=8, align_bytes=64)
-            if engine == "scalar":
-                nc.scalar.copy(out=res[:], in_=accs[h, m][:])
+        def store(h, m):
+            result = ring.tile([P, HALF], F32, name="result", tag="result", bufs=HALVES * M_TILES, align_bytes=64)
+            if m % 2 == 0:
+                nc.vector.tensor_copy(out=result[:], in_=acc[h, m][:])
             else:
-                nc.vector.tensor_copy(out=res[:], in_=accs[h, m][:])
-            nc.sync.dma_start(out=out[P * m : P * (m + 1), h * JH : (h + 1) * JH], in_=res[:])
+                nc.scalar.copy(out=result[:], in_=acc[h, m][:])
+            nc.sync.dma_start(out=out[P * m : P * (m + 1), h * HALF : (h + 1) * HALF], in_=result[:])
 
-        interleave_chars(0, 0, 0)
-        interleave_chars(0, 0, 1)
-        for n in range(6):
+        group_chars(0, 0, 0)
+        group_chars(0, 0, 1)
+        for n in range(HEAD_TILES):
             if n == 3:
                 quant_chars(0, 0)
             if n == 4:
                 quant_tastes(0)
-            widen(n, 2 if n == 0 else 1)
-            if n < 5:
+            widen(n, parts=2 if n == 0 else 1)
+            if n < HEAD_TILES - 1:
                 turn(n)
-                gather(n)
-            if n in (1, 2):
-                interleave_chars(1, 0, n - 1)
+                take_turned(n)
             if n == 0:
-                turn_weights()
+                take_inv()
             if n == 1:
-                split_weights()
+                split_inv()
+                group_chars(1, 0, 0)
             if n == 2:
-                scale_exponents()
-                spread_delta()
+                group_chars(1, 0, 1)
+                scale_exponent()
+                nc.scalar.copy(out=delta_all[:].bitcast(F32).rearrange("p (n i) -> p n i", i=PACK), in_=delta_rows)
             if n == 3:
-                join_logs()
+                join_ln()
             if n == 4:
                 nc.scalar.activation(scrap[:], one[:], ACT.Exp)
                 quant_chars(1, 0)
@@ -288,52 +309,53 @@ def tile_blp_choice_micro_moments_s13_kernel(
         first_product(0)
         first_product(1)
 
-        nxt = 2
-        for s in range(32):
-            if s < 28:
-                add_logs(s)
-            elif s < 28 + len(FINE):
-                lo, hi = FINE[s - 28]
-                for i in range(4):
-                    add_logs(28 + i, lo, hi)
-            for i in range(10):
-                if WIDEN_AT[i] == s:
-                    widen(6 + i)
-            for i in range(6):
-                if QUANT_TASTES_AT[i] == s:
-                    quant_tastes(2 + i)
-            for g in range(2):
-                if QUANT_CHARS_AT[g] == s:
+        made = 2
+        for s in range(CYCLES):
+            if s < FIRST_PIECE:
+                add_logs(s, 0, HALF)
+            elif s < FIRST_PIECE + len(PIECES):
+                for t in range(4):
+                    add_logs(FIRST_PIECE + t, *PIECES[s - FIRST_PIECE])
+            for n in range(HEAD_TILES, TILES):
+                if s == n - HEAD_TILES + late(n):
+                    widen(n)
+            for q in range(2, TILES // 2):
+                if s == 2 * q - 3 + late(2 * q):
+                    quant_tastes(q)
+            if s == CHARS_QUANT_CYCLE:
+                for g in range(K_PASSES):
                     quant_chars(g, 1)
-            for b in range(8):
-                for i in range(len(QUANT_SHARE_AT[b])):
-                    if QUANT_SHARE_AT[b][i] == s:
-                        lo, hi = FINE[i] if b == 7 else (0, JH)
-                        quant_share(b, lo, hi)
-            for i in range(11):
-                if TURN_AT[i] == s:
-                    turn(5 + i)
-            for b in range(8):
-                for m in range(4):
-                    if SECOND_AT[b][m] == s:
-                        second_product(b, m)
-            target = s + AHEAD[0] if s < AHEAD[1] else s + AHEAD[2]
-            while nxt <= min(target, 31):
-                first_product(nxt)
-                nxt += 1
-            for b in range(8):
-                for i in range(len(EXP_AT[b])):
-                    if EXP_AT[b][i] == s:
-                        lo, hi = FINE[i] if b == 7 else (256 * i, 256 * (i + 1))
-                        exponentiate(b, lo, hi)
-            for i in range(11):
-                if TURN_AT[i] == s:
-                    gather(5 + i)
+            for b in range(LAST):
+                if s == QUANT_CYCLE[b]:
+                    quant_share(b, 0, HALF)
+            for i in range(len(PIECES)):
+                if s == LAST_QUANT_CYCLE[i]:
+                    quant_share(LAST, *PIECES[i])
+            turning = [n for n in range(HEAD_TILES - 1, TILES) if s == n - HEAD_TILES + 1 + late(n)]
+            for n in turning:
+                turn(n)
+            for b in range(LAST):
+                if s == QUANT_CYCLE[b] + 1:
+                    second_product(b)
+            if s == CYCLES - 1:
+                second_product(LAST)
+            ahead = 2 if s < TILES - 1 else 4
+            while made < min(s + ahead + 1, UNITS):
+                first_product(made)
+                made += 1
+            for b in range(LAST):
+                if s == EXP_CYCLE[b]:
+                    exponentiate(b, 0, HALF)
+            for i in range(len(PIECES)):
+                if s == LAST_EXP_CYCLE[i]:
+                    exponentiate(LAST, *PIECES[i])
+            for n in turning:
+                take_turned(n)
             for i in range(4):
-                if CI_AT[i] == s:
-                    interleave_chars(i // 2, 1, i % 2)
-            for m in range(4):
-                if EVAC_AT[m] == s:
-                    store(0, m, "scalar" if EVAC_ON[m] == "S" else "vector")
-        for m in range(4):
-            store(1, m, "scalar" if m % 2 else "vector")
+                if s == CHARS_COPY_CYCLE[i]:
+                    group_chars(i // 2, 1, i % 2)
+            for m in range(M_TILES):
+                if s == STORE_CYCLE[m]:
+                    store(0, m)
+        for m in range(M_TILES):
+            store(1, m)

import math
from contextlib import ExitStack

import concourse.mybir as mybir
from concourse.masks import make_identity

C, K, J, M = 2048, 1024, 1024, 512
FLOPS = 2 * C * K * J + 2 * C * M * J

F32 = mybir.dt.float32
BF16 = mybir.dt.bfloat16
I32 = mybir.dt.int32
U32 = mybir.dt.uint32
U8 = mybir.dt.uint8
E4M3 = mybir.dt.float8_e4m3fn
E4M3X4 = mybir.dt.float8_e4m3fn_x4
E2M1X4 = mybir.dt.float4_e2m1fn_x4
ALU = mybir.AluOpType
ACT = mybir.ActivationFunctionType

P = 128
PACK = 4
PASS = P * PACK
HALF = 512
HALVES = J // HALF
GROUPS = C // PASS
TILES = C // P
K_PASSES = K // PASS
M_TILES = M // P
UNITS = HALVES * TILES
LN2 = math.log(2.0)

PIECES = ((0, 256), (256, 384), (384, HALF))
FIRST_PIECE = UNITS - 4
CYCLES = UNITS
LAST = HALVES * GROUPS - 1

HEAD_TILES = 6
LATE_TILE = 14

EXP_CYCLE = (5, 9, 13, 17, 20, 24, 28)
QUANT_CYCLE = (7, 11, 17, 19, 27, 27, 29)
LAST_EXP_CYCLE = (28, 29, 30)
LAST_QUANT_CYCLE = (30, 31, 31)
CHARS_COPY_CYCLE = (0, 1, 2, 3)
CHARS_QUANT_CYCLE = 13
STORE_CYCLE = (22, 22, 23, 23)


def late(n):
    return 1 if n >= LATE_TILE else 0


def tile_blp_choice_micro_moments_s13_kernel(
    tc, tastes_bytes, tastes_scale, chars, delta, inv_denom, demo_words, demo_scales, out
):
    nc = tc.nc
    with ExitStack() as ctx:
        keep = ctx.enter_context(tc.tile_pool(name="keep", bufs=1))
        ring = ctx.enter_context(tc.tile_pool(name="ring", bufs=2))
        psum = ctx.enter_context(tc.psum_pool(name="psum", bufs=1))
        ctx.enter_context(tc.manual_schedule())


        one = keep.tile([P, 1], F32, name="one")
        nc.vector.memset(one[:], 1.0)
        inv_rows = keep.tile([P, PASS // 2], F32, name="inv_rows", align_bytes=64)
        nc.vector.memset(inv_rows[:], 0.0)
        scale_cols = keep.tile([P, K_PASSES, PACK], F32, name="scale_cols")
        delta_cols = keep.tile([P, PACK], F32, name="delta_cols")
        ident = keep.tile([P, P], F32, name="ident")
        make_identity(nc, ident[:])
        demo_planes = keep.tile([P, GROUPS, M], U8, name="demo_planes", align_bytes=64)
        nc.gpsimd.memset(demo_planes[:].rearrange("p g m -> p (g m)").bitcast(I32), 0)

        tastes_view = tastes_bytes.rearrange("(g p t) k -> g p t k", p=P, t=PACK)
        chars_view = chars.rearrange("(g p t) j -> g p t j", p=P, t=PACK)
        tastes_raw = [keep.tile([P, PACK, K], U8, name="tastes_raw%d" % g, align_bytes=64) for g in range(GROUPS)]
        chars_raw = [
            [keep.tile([P, PACK, HALF], BF16, name="chars_raw%d%d" % (g, h), align_bytes=64) for h in range(HALVES)]
            for g in range(K_PASSES)
        ]
        demo_codes = keep.tile([P, GROUPS, 2 * M], U8, name="demo_codes", align_bytes=64)

        nc.sync.dma_start(out=scale_cols[:], in_=tastes_scale.rearrange("o (h n i) -> (o n) h i", h=K_PASSES, i=PACK))
        nc.sync.dma_start(out=tastes_raw[0][:, 0:1, :], in_=tastes_view[0][:, 0:1, :])
        nc.sync.dma_start(out=inv_rows[0:GROUPS, :].bitcast(BF16), in_=inv_denom.rearrange("(g r) -> g r", g=GROUPS))
        nc.sync.dma_start(out=delta_cols[:].bitcast(BF16), in_=delta.rearrange("(n i) -> n i", i=2 * PACK))
        nc.sync.dma_start(out=chars_raw[0][0][:], in_=chars_view[0][:, :, 0:HALF])
        nc.sync.dma_start(out=tastes_raw[0][:, 1:PACK, :], in_=tastes_view[0][:, 1:PACK, :])
        nc.sync.dma_start(out=chars_raw[1][0][:], in_=chars_view[1][:, :, 0:HALF])
        nc.sync.dma_start(out=tastes_raw[1][:], in_=tastes_view[1])
        nc.sync.dma_start(out=chars_raw[0][1][:], in_=chars_view[0][:, :, HALF:J])
        nc.sync.dma_start(out=chars_raw[1][1][:], in_=chars_view[1][:, :, HALF:J])
        nc.sync.dma_start(out=tastes_raw[2][:], in_=tastes_view[2])
        nc.sync.dma_start(out=tastes_raw[3][:], in_=tastes_view[3])
        nc.sync.dma_start(
            out=demo_codes[:].rearrange("p g n -> p (g n)").bitcast(I32).rearrange("p (g n) -> p g n", g=GROUPS),
            in_=demo_words.bitcast(I32).rearrange("g p n -> p g n"),
        )
        for q in range(4):
            nc.sync.dma_start(
                out=demo_planes[32 * q : 32 * q + 4, :, :]
                .rearrange("p g m -> p (g m)")
                .bitcast(I32)
                .rearrange("p (g m) -> p g m", g=GROUPS),
                in_=demo_scales.bitcast(I32).rearrange("g q m -> q g m")[4 * q : 4 * q + 4, :, :],
            )

        def spread(columns, tag):
            x = psum.tile([P, PACK, P], F32, name="spread", tag=tag, bufs=1)
            for i in range(PACK):
                nc.tensor.transpose(x[:, i, :], columns[:, i : i + 1].to_broadcast([P, P]), ident[:])
            return x[:].rearrange("p i n -> p n i")

        scrap = keep.tile([P, 1], F32, name="scrap")
        nc.scalar.activation(scrap[:], one[:], ACT.Ln)

        scale = keep.tile([P, K], F32, name="scale", align_bytes=64)
        scale_rows = [spread(scale_cols[:, g, :], "acc%d" % g) for g in range(K_PASSES)]
        nc.vector.tensor_copy(out=scale[:, 0:PASS].rearrange("p (n i) -> p n i", i=PACK), in_=scale_rows[0])
        nc.scalar.copy(out=scale[:, PASS:K].rearrange("p (n i) -> p n i", i=PACK), in_=scale_rows[1])

        inv_t = psum.tile([P, 2, P], F32, name="inv_t", tag="acc3", bufs=1)
        for u in range(2):
            nc.tensor.transpose(inv_t[:, u, :], inv_rows[:, u : PASS // 2 : 2], ident[:])

        delta_rows = spread(delta_cols[:], "acc2")
        delta_all = keep.tile([P, J], BF16, name="delta_all", align_bytes=64)

        inv = keep.tile([P, TILES], F32, name="inv")
        exponent = keep.tile([P, TILES], I32, name="exponent")
        significand = keep.tile([P, TILES], I32, name="significand")
        ln_significand = keep.tile([P, TILES], F32, name="ln_significand")
        ln_exponent = keep.tile([P, TILES], F32, name="ln_exponent")
        ln_inv = keep.tile([P, TILES], F32, name="ln_inv")

        def take_inv():
            nc.vector.tensor_copy(
                out=inv[:].rearrange("p (g u e) -> p u g e", u=2, e=2),
                in_=inv_t[:, :, 0:GROUPS].bitcast(BF16).rearrange("p u (g e) -> p u g e", e=2),
            )

        def split_inv():
            bits = inv[:].bitcast(I32)
            nc.vector.tensor_scalar(significand[:], bits, 0x7FFFFF, 0x3F800000, ALU.bitwise_and, ALU.bitwise_or)
            nc.vector.tensor_scalar(exponent[:], bits, 23, None, ALU.logical_shift_right)
            nc.scalar.activation(ln_significand[:], significand[:].bitcast(F32), ACT.Ln)

        def scale_exponent():
            nc.vector.tensor_scalar(ln_exponent[:], exponent[:], -127.0, LN2, ALU.add, ALU.mult)

        def join_ln():
            nc.vector.tensor_tensor(ln_inv[:], ln_significand[:], ln_exponent[:], ALU.add)

        widened, turned, pairs = {}, {}, {}
        tastes_codes = [keep.tile([P, 2 * K // PACK], U32, name="tastes_codes%d" % q, align_bytes=64) for q in range(TILES // 2)]
        tastes_planes = [keep.tile([P, 2 * K // PACK], U8, name="tastes_planes%d" % q, align_bytes=64) for q in range(TILES // 2)]

        def widen(n, parts=1):
            w = ring.tile([P, K], BF16, name="widened", tag="widened", bufs=4, align_bytes=64)
            for i in range(parts):
                cols = slice(K // parts * i, K // parts * (i + 1))
                nc.vector.tensor_tensor(w[:, cols], tastes_raw[n // 4][:, n % 4, cols].bitcast(E4M3), scale[:, cols], ALU.mult)
            widened[n] = w

        def turn(n):
            x = psum.tile([P, K_PASSES, 2, P], F32, name="turned", tag="xt", bufs=2)
            words = widened[n][:].bitcast(F32)
            for g in range(K_PASSES):
                for u in range(2):
                    nc.tensor.transpose(x[:, g, u, :], words[:, PASS // 2 * g + u : PASS // 2 * (g + 1) : 2], ident[:])
            turned[n] = x

        def take_turned(n):
            q, e = divmod(n, 2)
            if e == 0:
                pairs[q] = ring.tile([P, 2 * K], BF16, name="pair", tag="pair", bufs=3, align_bytes=64)
            dst = pairs[q][:, e * K : (e + 1) * K].bitcast(F32).rearrange("p (g r u) -> p g r u", g=K_PASSES, u=2)
            nc.scalar.copy(out=dst, in_=turned[n][:].rearrange("p g u r -> p g r u"))

        def quant_tastes(q):
            nc.vector.quantize_mx(out=tastes_codes[q][:].bitcast(E4M3X4), scales=tastes_planes[q][:], in_=pairs[q][:])

        def per_chars(name, shape, dtype):
            return [
                [keep.tile(shape, dtype, name="%s%d%d" % (name, g, h), align_bytes=64) for h in range(HALVES)]
                for g in range(K_PASSES)
            ]

        chars_grouped = per_chars("chars_grouped", [P, HALF, PACK], BF16)
        chars_codes = per_chars("chars_codes", [P, HALF], U32)
        chars_planes = per_chars("chars_planes", [P, HALF], U8)

        def interleave(engine_op, dst, src):
            engine_op(dst.rearrange("p (c i) t -> p c t i", i=4), src.rearrange("p t (c i) -> p c t i", i=4))

        def group_chars(g, h, part):
            cols = slice(256 * part, 256 * (part + 1))
            interleave(lambda o, i: nc.scalar.copy(out=o, in_=i), chars_grouped[g][h][:, cols, :], chars_raw[g][h][:, :, cols])

        def quant_chars(g, h):
            nc.vector.quantize_mx(
                out=chars_codes[g][h][:].bitcast(E4M3X4),
                scales=chars_planes[g][h][:],
                in_=chars_grouped[g][h][:].rearrange("p j t -> p (j t)"),
            )

        mu, logs, share, share_mx, acc = {}, {}, {}, {}, {}

        def first_product(s):
            h, n = divmod(s, TILES)
            tag = "xt" if h == 1 and s % 4 < 2 else "mu"
            mu[s] = psum.tile([P, HALF], F32, name="mu", tag=tag, bufs=2)
            q, e = divmod(n, 2)
            for g in range(K_PASSES):
                cols = slice(K // PACK * e + P * g, K // PACK * e + P * (g + 1))
                nc.tensor.matmul_mx(
                    out=mu[s][:],
                    lhsT=tastes_codes[q][:, cols].bitcast(E4M3X4),
                    lhsT_scale=tastes_planes[q][:, cols],
                    rhs=chars_codes[g][h][:].bitcast(E4M3X4),
                    rhs_scale=chars_planes[g][h][:],
                    start=(g == 0),
                    stop=(g == K_PASSES - 1),
                )

        def add_logs(s, lo, hi):
            h, n = divmod(s, TILES)
            b, t = divmod(s, 4)
            if t == 0:
                logs[b, lo] = ring.tile(
                    [P, 4, hi - lo], F32, name="logs", tag="logs%d" % (hi - lo), bufs=3 if hi - lo == HALF else 2, align_bytes=64
                )
            nc.vector.scalar_tensor_tensor(
                out=logs[b, lo][:, t, :],
                in0=mu[s][:, lo:hi],
                scalar=ln_inv[:, n : n + 1],
                in1=delta_all[:, h * HALF + lo : h * HALF + hi],
                op0=ALU.add,
                op1=ALU.add,
            )

        def exponentiate(b, lo, hi):
            if lo == 0:
                share[b] = ring.tile([P, HALF, PACK], BF16, name="share", tag="share", bufs=3, align_bytes=64)
            interleave(lambda o, i: nc.scalar.activation(o, i, ACT.Exp), share[b][:, lo:hi, :], logs[b, lo][:])

        def quant_share(b, lo, hi):
            if lo == 0:
                codes = ring.tile([P, HALF], U32, name="share_codes", tag="share_codes", bufs=3, align_bytes=64)
                planes = ring.tile([P, HALF], U8, name="share_planes", tag="share_planes", bufs=3, align_bytes=64)
                share_mx[b] = (codes, planes)
            codes, planes = share_mx[b]
            nc.vector.quantize_mx(
                out=codes[:, lo:hi].bitcast(E4M3X4), scales=planes[:, lo:hi], in_=share[b][:, lo:hi, :].rearrange("p j t -> p (j t)")
            )

        def second_product(b):
            h, g = divmod(b, GROUPS)
            codes, planes = share_mx[b]
            for m in range(M_TILES):
                if g == 0:
                    acc[h, m] = psum.tile([P, HALF], F32, name="acc", tag="acc%d" % m, bufs=1)
                nc.tensor.matmul_mx(
                    out=acc[h, m][:],
                    lhsT=demo_codes[:, g, 2 * P * m : 2 * P * (m + 1)].bitcast(E2M1X4),
                    lhsT_scale=demo_planes[:, g, P * m : P * (m + 1)],
                    rhs=codes[:].bitcast(E4M3X4),
                    rhs_scale=planes[:],
                    start=(g == 0),
                    stop=(g == GROUPS - 1),
                )

        def store(h, m):
            result = ring.tile([P, HALF], F32, name="result", tag="result", bufs=HALVES * M_TILES, align_bytes=64)
            if m % 2 == 0:
                nc.vector.tensor_copy(out=result[:], in_=acc[h, m][:])
            else:
                nc.scalar.copy(out=result[:], in_=acc[h, m][:])
            nc.sync.dma_start(out=out[P * m : P * (m + 1), h * HALF : (h + 1) * HALF], in_=result[:])

        group_chars(0, 0, 0)
        group_chars(0, 0, 1)
        for n in range(HEAD_TILES):
            if n == 3:
                quant_chars(0, 0)
            if n == 4:
                quant_tastes(0)
            widen(n, parts=2 if n == 0 else 1)
            if n < HEAD_TILES - 1:
                turn(n)
                take_turned(n)
            if n == 0:
                take_inv()
            if n == 1:
                split_inv()
                group_chars(1, 0, 0)
            if n == 2:
                group_chars(1, 0, 1)
                scale_exponent()
                nc.scalar.copy(out=delta_all[:].bitcast(F32).rearrange("p (n i) -> p n i", i=PACK), in_=delta_rows)
            if n == 3:
                join_ln()
            if n == 4:
                nc.scalar.activation(scrap[:], one[:], ACT.Exp)
                quant_chars(1, 0)
        quant_tastes(1)
        first_product(0)
        first_product(1)

        made = 2
        for s in range(CYCLES):
            if s < FIRST_PIECE:
                add_logs(s, 0, HALF)
            elif s < FIRST_PIECE + len(PIECES):
                for t in range(4):
                    add_logs(FIRST_PIECE + t, *PIECES[s - FIRST_PIECE])
            for n in range(HEAD_TILES, TILES):
                if s == n - HEAD_TILES + late(n):
                    widen(n)
            for q in range(2, TILES // 2):
                if s == 2 * q - 3 + late(2 * q):
                    quant_tastes(q)
            if s == CHARS_QUANT_CYCLE:
                for g in range(K_PASSES):
                    quant_chars(g, 1)
            for b in range(LAST):
                if s == QUANT_CYCLE[b]:
                    quant_share(b, 0, HALF)
            for i in range(len(PIECES)):
                if s == LAST_QUANT_CYCLE[i]:
                    quant_share(LAST, *PIECES[i])
            turning = [n for n in range(HEAD_TILES - 1, TILES) if s == n - HEAD_TILES + 1 + late(n)]
            for n in turning:
                turn(n)
            for b in range(LAST):
                if s == QUANT_CYCLE[b] + 1:
                    second_product(b)
            if s == CYCLES - 1:
                second_product(LAST)
            ahead = 2 if s < TILES - 1 else 4
            while made < min(s + ahead + 1, UNITS):
                first_product(made)
                made += 1
            for b in range(LAST):
                if s == EXP_CYCLE[b]:
                    exponentiate(b, 0, HALF)
            for i in range(len(PIECES)):
                if s == LAST_EXP_CYCLE[i]:
                    exponentiate(LAST, *PIECES[i])
            for n in turning:
                take_turned(n)
            for i in range(4):
                if s == CHARS_COPY_CYCLE[i]:
                    group_chars(i // 2, 1, i % 2)
            for m in range(M_TILES):
                if s == STORE_CYCLE[m]:
                    store(0, m)
        for m in range(M_TILES):
            store(1, m)
